import numpy as np
import ml_dtypes


def mxq(x, axis, fmt="e4m3"):
    dtype, down = {"e4m3": (ml_dtypes.float8_e4m3fn, 7), "e5m2": (ml_dtypes.float8_e5m2, 14)}[fmt]
    v = np.moveaxis(np.asarray(x, np.float32).astype(ml_dtypes.bfloat16).astype(np.float64), axis, -1)
    blocks = v.reshape(v.shape[:-1] + (-1, 32))
    amax = np.abs(blocks).max(-1, keepdims=True)
    byte = np.maximum(np.where(amax > 0, np.frexp(amax)[1] - 1 + 127, 0) - down, 1)
    scale = np.exp2(byte - 127.0)
    codes = (blocks / scale).astype(np.float32).astype(dtype).astype(np.float64)
    return np.moveaxis((codes * scale).reshape(v.shape), -1, axis)


WIDE = False


def mx_kscale(k):
    if not WIDE:
        return np.ones(k)
    levels = np.array([10, -10, 5, -5, 0])
    if k % 512:
        return np.exp2(np.random.permutation(np.resize(levels, k // 32))).repeat(32)
    a = np.empty((k // 512, 16))
    for p in range(k // 512):
        a[p, :8] = np.random.permutation(np.resize(levels, 8))
        for g in range(8):
            far = levels[np.abs(levels - a[p, g]) >= 10]
            a[p, g + 8] = far[np.random.randint(len(far))]
    return np.exp2(a.ravel()).repeat(32)


BF16 = ml_dtypes.bfloat16


def bf(x):
    return np.asarray(x, np.float32).astype(BF16)


def f64(x):
    return np.asarray(x).astype(np.float64)


B, D, T, P, Q = 32, 512, 512, 128, 128


def scaled_softmax(e):
    p = np.exp(e - e.max(axis=-1, keepdims=True))
    return e.shape[-1] * (p / p.sum(axis=-1, keepdims=True))


def draw0():
    s, t = mx_kscale(D), mx_kscale(T)
    return {
        "x": bf(np.random.standard_normal((B, D, T)) * s[None, :, None]),
        "w1": bf(np.random.standard_normal((P, D)) / np.sqrt(D) / s[None, :]),
        "g": bf((1.0 + 0.1 * np.random.standard_normal(T)) * t),
        "w": bf(np.random.standard_normal((T, Q)) / np.sqrt(T) / t[:, None]),
        "w2": bf(np.random.standard_normal((T, Q)) / np.sqrt(T) / t[:, None]),
        "lam": bf(np.random.uniform(0.3, 0.7, P)),
        "bias": bf(0.4 * np.random.standard_normal((P, Q))),
    }


def core(x, w1, g, w, w2, lam, bias):
    h0 = mxq(f64(w1), 1, "e4m3") @ mxq(f64(x), 1, "e4m3")
    h = h0 * f64(g)[None, None, :]
    hq = mxq(h, 2, "e4m3")
    u = hq @ mxq(f64(w2), 0, "e4m3")
    e = hq @ mxq(f64(w), 0, "e4m3")
    a = scaled_softmax(e)
    mix = f64(lam)[None, :, None]
    z = mix * u * a + (1.0 - mix) * u + f64(bias)[None, :, :]
    return np.tanh(z)


def e4m3fn_bytes(y):
    return np.clip(np.asarray(y, np.float64), -448.0, 448.0).astype(np.float32).astype(ml_dtypes.float8_e4m3fn).view(np.uint8)


def e4m3fn_values(b):
    return np.asarray(b, np.uint8).view(ml_dtypes.float8_e4m3fn).astype(np.float64)


def setup_inputs():
    d = draw0()
    x0 = np.asarray(d['x']).astype(np.float64)
    s = (np.max(np.abs(x0), axis=(0, 2), keepdims=True) / 448.0).astype(np.float32)
    out = {}
    for k, v in d.items():
        if k == 'x':
            out['x_bytes'] = e4m3fn_bytes(x0 / s.astype(np.float64))
            out['x_scale'] = s
        else:
            out[k] = v
    return out


def reference(x_bytes, x_scale, w1, g, w, w2, lam, bias):
    return core(e4m3fn_values(x_bytes) * x_scale.astype(np.float64), w1, g, w, w2, lam, bias)

@@ -1,0 +1,370 @@
+from contextlib import ExitStack
+
+import concourse.mybir as mybir
+from concourse.masks import make_identity
+
+B, D, T, PF, Q = 32, 512, 512, 128, 128
+FLOPS = 2 * B * PF * D * T + 2 * 2 * B * PF * T * Q
+
+F32 = mybir.dt.float32
+BF16 = mybir.dt.bfloat16
+U32 = mybir.dt.uint32
+U8 = mybir.dt.uint8
+FP8 = mybir.dt.float8_e4m3fn
+FP8X4 = mybir.dt.float8_e4m3fn_x4
+ALU = mybir.AluOpType
+ACT = mybir.ActivationFunctionType
+AX = mybir.AxisListType
+
+P = 128
+AHEAD = 5
+LOAD_AHEAD = 10
+
+
+def shares(n):
+    if n < 2:
+        return 32, 0, 0, 0
+    if n >= 28:
+        return 2, 20, 4, 6
+    if n % 2 == 0:
+        return 20, 0, 4, 8
+    return 22, 0, 4, 6
+
+
+def tile_temporalaugmentedbilinear_t_kernel(tc, x_bytes, x_scale, w1, g, w, w2, lam, bias, out):
+    nc = tc.nc
+    with ExitStack() as ctx:
+        keep = ctx.enter_context(tc.tile_pool(name="keep", bufs=1))
+        raws = ctx.enter_context(tc.tile_pool(name="raws", bufs=6))
+        pln = ctx.enter_context(tc.tile_pool(name="pln", bufs=4))
+        grp = ctx.enter_context(tc.tile_pool(name="grp", bufs=3))
+        cod = ctx.enter_context(tc.tile_pool(name="cod", bufs=3))
+        hp = ctx.enter_context(tc.tile_pool(name="hp", bufs=2))
+        ep = ctx.enter_context(tc.tile_pool(name="ep", bufs=4))
+        ps_h = ctx.enter_context(tc.psum_pool(name="ps_h", bufs=3))
+        ps_ue = ctx.enter_context(tc.psum_pool(name="ps_ue", bufs=3))
+        ps_i = ctx.enter_context(tc.psum_pool(name="ps_i", bufs=2))
+        ctx.enter_context(tc.manual_schedule())
+
+        raw = {}
+
+        def load(b):
+            if b >= B:
+                return
+            q = b // 2
+            if b % 2 == 0:
+                raw[q] = raws.tile([P, 4, 2, T], U8, name="raw", align_bytes=64)
+            rows = x_bytes[b].rearrange("(p i) t -> p i t", i=4)
+            for i in ((2, 0) if b == 0 else (0,)):
+                k = 2 if b == 0 else 4
+                nc.sync.dma_start(out=raw[q][:, i : i + k, b % 2, :], in_=rows[:, i : i + k])
+
+        xs = keep.tile([P, 4], F32, name="xs")
+        nc.sync.dma_start(out=xs[:], in_=x_scale.rearrange("o (p i) z -> p (o i z)", i=4))
+        load(0)
+
+        w1_sb = keep.tile([P, D], BF16, name="w1_sb", align_bytes=64)
+        w_sb = keep.tile([P, 2, 4, Q], BF16, name="w_sb", align_bytes=64)
+        g_sb = keep.tile([P, 4], BF16, name="g_sb")
+        lam_sb = keep.tile([P, 1], BF16, name="lam_sb")
+        bias_sb = keep.tile([P, Q], BF16, name="bias_sb")
+        nc.sync.dma_start(out=w1_sb[:], in_=w1)
+        load(1)
+        g_rows = keep.tile([P, P], BF16, name="g_rows", align_bytes=64)
+        nc.gpsimd.memset(g_rows[:], 0.0)
+        nc.scalar.dma_start(
+            out=g_rows[0:4, :].rearrange("j (s r) -> j s r", r=4), in_=g.rearrange("(s j r) -> j s r", j=4, r=4)
+        )
+        nc.scalar.dma_start(out=lam_sb[:], in_=lam.rearrange("(p o) -> p o", o=1))
+        for b in range(2, 6):
+            load(b)
+        nc.sync.dma_start(out=bias_sb[:], in_=bias)
+        for k, wt in enumerate((w2, w)):
+            rows = wt.rearrange("(s j r) q -> r s j q", j=4, r=4)
+            for r in range(4):
+                nc.sync.dma_start(out=w_sb[r:P:4, k], in_=rows[r])
+        for b in range(6, LOAD_AHEAD):
+            load(b)
+
+        warm = keep.tile([P, 1], F32, name="warm")
+        nc.gpsimd.memset(warm[:], 0.0)
+        nc.scalar.activation(out=warm[:], in_=warm[:], func=ACT.Exp)
+
+        ident = keep.tile([P, P], F32, name="ident")
+        make_identity(nc, ident[:])
+        ident_b = keep.tile([P, P], BF16, name="ident_b", align_bytes=64)
+        nc.gpsimd.tensor_copy(out=ident_b[:], in_=ident[:])
+
+        planes = {}
+
+        def new_planes(q):
+            planes[q] = pln.tile([P, 4, 2, T], BF16, name="planes", align_bytes=64)
+
+        def widen_half(h):
+            if h >= B:
+                return
+            q = h // 2
+            if h % 2 == 0:
+                new_planes(q)
+            for i in (2 * (h % 2), 2 * (h % 2) + 1):
+                wide = planes[q][:, i].rearrange("p b t -> p (b t)")
+                codes = raw[q][:, i].rearrange("p b t -> p (b t)").bitcast(FP8)
+                if (q == 1 and i % 2) or (q % 4 == 3 and i == 3):
+                    nc.vector.tensor_scalar(out=wide, in0=codes, scalar1=xs[:, i : i + 1], scalar2=None, op0=ALU.mult)
+                else:
+                    nc.scalar.activation(out=wide, in_=codes, func=ACT.Copy, scale=xs[:, i : i + 1])
+
+        new_planes(0)
+        for b in (0, 1):
+            for i in range(4):
+                if i < 2:
+                    nc.vector.tensor_scalar(
+                        out=planes[0][:, i, b, :], in0=raw[0][:, i, b, :].bitcast(FP8),
+                        scalar1=xs[:, i : i + 1], scalar2=None, op0=ALU.mult,
+                    )
+                else:
+                    nc.scalar.activation(
+                        out=planes[0][:, i, b, :], in_=raw[0][:, i, b, :].bitcast(FP8),
+                        func=ACT.Copy, scale=xs[:, i : i + 1],
+                    )
+        for h in range(2, AHEAD):
+            widen_half(h)
+
+        w1_words = w1_sb[:].bitcast(F32)
+        w1_t = ps_h.tile([P, 512], F32, name="h_ps")
+        for u in (0, 1):
+            nc.tensor.transpose(w1_t[:, 128 * u : 128 * (u + 1)], w1_words[:, u : 256 : 2], ident[:])
+        w1_g = keep.tile([P, 512], BF16, name="w1_g", align_bytes=64)
+        w1_c = keep.tile([P, 128], U32, name="w1_c", align_bytes=64)
+        w1_s = keep.tile([P, 128], U8, name="w1_s", align_bytes=64)
+        w_g = keep.tile([P, 2, Q, 4], BF16, name="w_g", align_bytes=64)
+        w_c = keep.tile([P, 256], U32, name="w_c", align_bytes=64)
+        w_s = keep.tile([P, 256], U8, name="w_s", align_bytes=64)
+
+        g_t = ps_i.tile([P, P], BF16, name="id_ps")
+        nc.tensor.transpose(g_t[:], g_rows[:], ident_b[:])
+
+        def prep_w1_copy():
+            nc.vector.tensor_copy(out=g_sb[:], in_=g_t[:, 0:4])
+            nc.vector.tensor_copy(
+                out=w1_g[:].bitcast(F32).rearrange("p (r u) -> p r u", u=2),
+                in_=w1_t[:, 0:256].rearrange("p (u r) -> p r u", u=2),
+            )
+
+        def prep_w1_quant():
+            nc.vector.quantize_mx(out=w1_c[:].bitcast(FP8X4), scales=w1_s[:], in_=w1_g[:])
+
+        def prep_w_copy():
+            nc.vector.tensor_copy(out=w_g[:, 0], in_=w_sb[:, 0].rearrange("p j q -> p q j"))
+            nc.vector.tensor_scalar(
+                out=w_g[:, 1], in0=w_sb[:, 1].rearrange("p j q -> p q j"),
+                scalar1=-1.0, scalar2=None, op0=ALU.mult,
+            )
+
+        def prep_w_quant():
+            nc.vector.quantize_mx(
+                out=w_c[:].bitcast(FP8X4), scales=w_s[:], in_=w_g[:].rearrange("p a q j -> p (a q j)")
+            )
+
+        lam_lo = keep.tile([P, 1], F32, name="lam_lo")
+        lam_hi = keep.tile([P, 1], F32, name="lam_hi")
+        c128 = keep.tile([P, 1], F32, name="c128")
+        oml = keep.tile([P, 1], F32, name="oml")
+        rc = keep.tile([P, 1], F32, name="rc")
+        coef = keep.tile([P, 2], F32, name="coef")
+        TINY = 1e-20
+
+        def prep_lam():
+            nc.gpsimd.tensor_scalar(out=lam_lo[:], in0=lam_sb[:], scalar1=TINY, scalar2=TINY, op0=ALU.is_lt, op1=ALU.mult)
+            nc.gpsimd.tensor_scalar(out=lam_hi[:], in0=lam_sb[:], scalar1=-TINY, scalar2=None, op0=ALU.is_gt)
+            nc.gpsimd.tensor_tensor(out=lam_lo[:], in0=lam_lo[:], in1=lam_hi[:], op=ALU.mult)
+            nc.gpsimd.tensor_tensor(out=c128[:], in0=lam_lo[:], in1=lam_sb[:], op=ALU.add)
+            nc.gpsimd.tensor_scalar(out=c128[:], in0=c128[:], scalar1=128.0, scalar2=None, op0=ALU.mult)
+            nc.gpsimd.tensor_scalar(out=oml[:], in0=lam_sb[:], scalar1=-1.0, scalar2=1.0, op0=ALU.mult, op1=ALU.add)
+            nc.vector.reciprocal(rc[:], c128[:])
+            nc.gpsimd.tensor_copy(out=coef[:, 0:1], in_=rc[:])
+            nc.gpsimd.tensor_tensor(out=coef[:, 1:2], in0=oml[:], in1=rc[:], op=ALU.mult)
+
+        grouped, xc, xsc = {}, {}, {}
+
+        def lay(n, part):
+            s = shares(n)
+            a0 = sum(s[:part])
+            a1 = a0 + s[part]
+            src = planes[n // 2][:, :, n % 2, :].rearrange("p i (s j r) -> p s j r i", j=4, r=4)
+            dst = grouped[n][:].rearrange("p j s r i -> p s j r i")
+            return src[:, a0:a1], dst[:, a0:a1]
+
+        def interleave_g(n):
+            if n >= B:
+                return
+            grouped[n] = grp.tile([P, 4, 32, 4, 4], BF16, name="grouped", align_bytes=64)
+            if shares(n)[3]:
+                src, dst = lay(n, 3)
+                nc.gpsimd.tensor_scalar(out=dst, in0=src, scalar1=1.0, scalar2=0.0, op0=ALU.mult, op1=ALU.add)
+
+        def interleave_v(n):
+            src, dst = (ap.rearrange("p s j r i -> p s j i r") for ap in lay(n, 0))
+            nc.vector.tensor_copy(out=dst, in_=src)
+
+        id_ps = {}
+
+        def interleave_t(n):
+            if n >= B or not shares(n)[2]:
+                return
+            src, dst = lay(n, 2)
+            id_ps[n] = ps_i.tile([P, 256], BF16, name="id_ps")
+            nc.tensor.matmul(
+                id_ps[n][:].rearrange("p (t i) -> p t i", i=4), lhsT=ident_b[:],
+                rhs=src.rearrange("p s j r i -> p (s j r) i"), start=True, stop=True,
+            )
+
+        def interleave_s(n):
+            if n >= B:
+                return
+            if shares(n)[2]:
+                src, dst = lay(n, 2)
+                nc.scalar.copy(
+                    out=dst.rearrange("p s j r i -> p s j (r i)"),
+                    in_=id_ps[n][:].rearrange("p (s j c) -> p s j c", j=4, c=16),
+                )
+            if shares(n)[1]:
+                src, dst = lay(n, 1)
+                nc.scalar.copy(out=dst, in_=src)
+
+        def quant(n):
+            xc[n] = cod.tile([P, 512], U32, name="xc", align_bytes=64)
+            xsc[n] = cod.tile([P, 512], U8, name="xsc", align_bytes=64)
+            nc.vector.quantize_mx(
+                out=xc[n][:].bitcast(FP8X4), scales=xsc[n][:],
+                in_=grouped[n][:].rearrange("p j s r i -> p (j s r i)"),
+            )
+
+        h_ps = {}
+
+        def mm1(n):
+            h_ps[n] = ps_h.tile([P, 512], F32, name="h_ps")
+            for j in range(4):
+                cols = slice(128 * j, 128 * (j + 1))
+                nc.tensor.matmul_mx(
+                    out=h_ps[n][:, cols],
+                    lhsT=xc[n][:, cols].bitcast(FP8X4), lhsT_scale=xsc[n][:, cols],
+                    rhs=w1_c[:].bitcast(FP8X4), rhs_scale=w1_s[:],
+                    start=True, stop=True,
+                )
+
+        hg, hc, hs = {}, {}, {}
+
+        def gain(n):
+            q = n // 2
+            if n % 2 == 0:
+                hg[q] = hp.tile([P, 2, PF, 4], BF16, name="hg", align_bytes=64)
+            nc.vector.tensor_tensor(
+                out=hg[q][:, n % 2],
+                in0=h_ps[n][:].rearrange("p (j f) -> p f j", j=4),
+                in1=g_sb[:].unsqueeze(1).to_broadcast([P, PF, 4]),
+                op=ALU.mult,
+            )
+
+        def hquant(q):
+            hc[q] = hp.tile([P, 2 * PF], U32, name="hc", align_bytes=64)
+            hs[q] = hp.tile([P, 2 * PF], U8, name="hs", align_bytes=64)
+            nc.vector.quantize_mx(
+                out=hc[q][:].bitcast(FP8X4), scales=hs[q][:], in_=hg[q][:].rearrange("p b f j -> p (b f j)")
+            )
+
+        ue = {}
+
+        def mm2(q):
+            ue[q] = ps_ue.tile([P, 2, 2, Q], F32, name="ue")
+            for r in (0, 1):
+                rows = slice(PF * r, PF * (r + 1))
+                nc.tensor.matmul_mx(
+                    out=ue[q][:, r].rearrange("p a q -> p (a q)"),
+                    lhsT=hc[q][:, rows].bitcast(FP8X4), lhsT_scale=hs[q][:, rows],
+                    rhs=w_c[:].bitcast(FP8X4), rhs_scale=w_s[:],
+                    start=True, stop=True,
+                )
+
+        mn, sm, fac, cc, ex = {}, {}, {}, {}, {}
+
+        def row_max(q):
+            mn[q] = ep.tile([P, 2], F32, name="mn")
+            nc.vector.tensor_reduce(out=mn[q][:], in_=ue[q][:, :, 1], axis=AX.X, op=ALU.min)
+
+        def exps(q):
+            sm[q] = ep.tile([P, 2], F32, name="sm")
+            ex[q] = ep.tile([P, 2, Q], F32, name="ex")
+            for r in (0, 1):
+                nc.scalar.activation(
+                    out=ex[q][:, r], in_=ue[q][:, r, 1], func=ACT.Exp,
+                    bias=mn[q][:, r : r + 1], scale=-1.0, accum_out=sm[q][:, r : r + 1],
+                )
+
+        def factors(q):
+            fac[q] = ep.tile([P, 2, 2], F32, name="fac")
+            nc.gpsimd.tensor_tensor(
+                out=fac[q][:], in0=sm[q][:].unsqueeze(1).to_broadcast([P, 2, 2]),
+                in1=coef[:].unsqueeze(2).to_broadcast([P, 2, 2]), op=ALU.mult,
+            )
+
+        def invert(q):
+            cc[q] = ep.tile([P, 2], F32, name="cc")
+            nc.vector.reciprocal(cc[q][:], fac[q][:, 0])
+
+        def weigh(q):
+            for r in (0, 1):
+                nc.vector.scalar_tensor_tensor(
+                    out=ex[q][:, r], in0=ex[q][:, r], scalar=fac[q][:, 1, r : r + 1], in1=ue[q][:, r, 0],
+                    op0=ALU.add, op1=ALU.mult,
+                )
+
+        def mix(q):
+            for r in (0, 1):
+                nc.vector.scalar_tensor_tensor(
+                    out=ex[q][:, r], in0=ex[q][:, r], scalar=cc[q][:, r : r + 1], in1=bias_sb[:],
+                    op0=ALU.mult, op1=ALU.add,
+                )
+
+        def finish(q):
+            o = ep.tile([P, 2, Q], F32, name="o")
+            nc.scalar.activation(out=o[:], in_=ex[q][:], func=ACT.Tanh)
+            nc.sync.dma_start(out=out[2 * q : 2 * q + 2].rearrange("b p q -> p b q"), in_=o[:])
+
+        def at(stage, lag, n):
+            if 0 <= n - lag < B and (n - lag) % 2 == 0:
+                stage((n - lag) // 2)
+
+        interleave_g(0)
+        interleave_g(1)
+        for n in range(B + 9):
+            load(n + LOAD_AHEAD)
+            if 0 <= n - 1 < B:
+                quant(n - 1)
+                mm1(n - 1)
+            if n < B:
+                interleave_v(n)
+            if n == 0:
+                prep_w1_copy()
+                prep_w1_quant()
+                prep_lam()
+            if n == 2:
+                prep_w_copy()
+            if n == 3:
+                prep_w_quant()
+            interleave_g(n + 2)
+            at(factors, 7, n)
+            interleave_t(n + 2)
+            interleave_s(n + 1)
+            if 0 <= n - 2 < B:
+                gain(n - 2)
+            at(invert, 8, n)
+            at(weigh, 8, n)
+            at(row_max, 5, n)
+            at(mix, 9, n)
+            if n + AHEAD < B:
+                widen_half(n + AHEAD)
+            at(exps, 6, n)
+            at(hquant, 4, n)
+            at(mm2, 4, n)
+            at(finish, 10, n)

@@ -17,123 +17,110 @@ ACT = mybir.ActivationFunctionType
 AX = mybir.AxisListType
 
 P = 128
-AHEAD = 5
-LOAD_AHEAD = 10
+PAIRS = B // 2
+RUNS = 32
+TENSOR_RUNS = 10
+LOAD_AHEAD = 4
+SCALAR_LAST_RUNS = 24
 
 
-def shares(n):
-    if n < 2:
-        return 32, 0, 0, 0
-    if n >= 28:
-        return 2, 20, 4, 6
-    if n % 2 == 0:
-        return 20, 0, 4, 8
-    return 22, 0, 4, 6
+def gpsimd_runs(q):
+    return {0: 0, 1: 10, 2: 14, PAIRS - 1: 20}.get(q, 22)
+
+
+def vector_widens(q):
+    room = 16 * gpsimd_runs(q)
+    return {2: min(0, room), 3: min(320, room)}
 
 
 def tile_temporalaugmentedbilinear_t_kernel(tc, x_bytes, x_scale, w1, g, w, w2, lam, bias, out):
     nc = tc.nc
     with ExitStack() as ctx:
         keep = ctx.enter_context(tc.tile_pool(name="keep", bufs=1))
-        raws = ctx.enter_context(tc.tile_pool(name="raws", bufs=6))
-        pln = ctx.enter_context(tc.tile_pool(name="pln", bufs=4))
-        grp = ctx.enter_context(tc.tile_pool(name="grp", bufs=3))
-        cod = ctx.enter_context(tc.tile_pool(name="cod", bufs=3))
+        raws = ctx.enter_context(tc.tile_pool(name="raws", bufs=LOAD_AHEAD + 1))
+        pln = ctx.enter_context(tc.tile_pool(name="pln", bufs=3))
+        grp = ctx.enter_context(tc.tile_pool(name="grp", bufs=2))
+        cod = ctx.enter_context(tc.tile_pool(name="cod", bufs=2))
         hp = ctx.enter_context(tc.tile_pool(name="hp", bufs=2))
         ep = ctx.enter_context(tc.tile_pool(name="ep", bufs=4))
-        ps_h = ctx.enter_context(tc.psum_pool(name="ps_h", bufs=3))
+        ps_h = ctx.enter_context(tc.psum_pool(name="ps_h", bufs=2))
         ps_ue = ctx.enter_context(tc.psum_pool(name="ps_ue", bufs=3))
         ps_i = ctx.enter_context(tc.psum_pool(name="ps_i", bufs=2))
+        ps_c = ctx.enter_context(tc.psum_pool(name="ps_c", bufs=1))
         ctx.enter_context(tc.manual_schedule())
 
         raw = {}
 
-        def load(b):
-            if b >= B:
+        def load(q):
+            if q >= PAIRS:
                 return
-            q = b // 2
-            if b % 2 == 0:
-                raw[q] = raws.tile([P, 4, 2, T], U8, name="raw", align_bytes=64)
-            rows = x_bytes[b].rearrange("(p i) t -> p i t", i=4)
-            for i in ((2, 0) if b == 0 else (0,)):
-                k = 2 if b == 0 else 4
-                nc.sync.dma_start(out=raw[q][:, i : i + k, b % 2, :], in_=rows[:, i : i + k])
+            raw[q] = raws.tile([P, 4, 2, T], U8, name="raw", align_bytes=64)
+            for r in (0, 1):
+                load_batch(q, r)
+
+        def load_batch(q, r, slots=slice(0, 4)):
+            rows = x_bytes[2 * q + r].rearrange("(p i) t -> p i t", i=4)
+            nc.sync.dma_start(out=raw[q][:, slots, r, :], in_=rows[:, slots])
 
         xs = keep.tile([P, 4], F32, name="xs")
-        nc.sync.dma_start(out=xs[:], in_=x_scale.rearrange("o (p i) z -> p (o i z)", i=4))
-        load(0)
-
         w1_sb = keep.tile([P, D], BF16, name="w1_sb", align_bytes=64)
         w_sb = keep.tile([P, 2, 4, Q], BF16, name="w_sb", align_bytes=64)
         g_sb = keep.tile([P, 4], BF16, name="g_sb")
         lam_sb = keep.tile([P, 1], BF16, name="lam_sb")
         bias_sb = keep.tile([P, Q], BF16, name="bias_sb")
+        g_rows = keep.tile([P, P], BF16, name="g_rows", align_bytes=64)
+
+        nc.scalar.dma_start(out=xs[:], in_=x_scale.rearrange("o (p i) z -> p (o i z)", i=4))
+        raw[0] = raws.tile([P, 4, 2, T], U8, name="raw", align_bytes=64)
+        load_batch(0, 0, slice(0, 2))
+        load_batch(0, 0, slice(2, 4))
+        load_batch(0, 1)
         nc.sync.dma_start(out=w1_sb[:], in_=w1)
         load(1)
-        g_rows = keep.tile([P, P], BF16, name="g_rows", align_bytes=64)
         nc.gpsimd.memset(g_rows[:], 0.0)
         nc.scalar.dma_start(
             out=g_rows[0:4, :].rearrange("j (s r) -> j s r", r=4), in_=g.rearrange("(s j r) -> j s r", j=4, r=4)
         )
         nc.scalar.dma_start(out=lam_sb[:], in_=lam.rearrange("(p o) -> p o", o=1))
-        for b in range(2, 6):
-            load(b)
+        load(2)
         nc.sync.dma_start(out=bias_sb[:], in_=bias)
         for k, wt in enumerate((w2, w)):
             rows = wt.rearrange("(s j r) q -> r s j q", j=4, r=4)
             for r in range(4):
                 nc.sync.dma_start(out=w_sb[r:P:4, k], in_=rows[r])
-        for b in range(6, LOAD_AHEAD):
-            load(b)
-
-        warm = keep.tile([P, 1], F32, name="warm")
-        nc.gpsimd.memset(warm[:], 0.0)
-        nc.scalar.activation(out=warm[:], in_=warm[:], func=ACT.Exp)
+        load(3)
 
         ident = keep.tile([P, P], F32, name="ident")
         make_identity(nc, ident[:])
         ident_b = keep.tile([P, P], BF16, name="ident_b", align_bytes=64)
-        nc.gpsimd.tensor_copy(out=ident_b[:], in_=ident[:])
+        nc.scalar.activation(out=ident_b[:], in_=ident[:], func=ACT.Copy)
 
         planes = {}
 
-        def new_planes(q):
-            planes[q] = pln.tile([P, 4, 2, T], BF16, name="planes", align_bytes=64)
+        def slot_views(q, i, lo, hi):
+            wide = planes[q][:, i].rearrange("p b t -> p (b t)")[:, lo:hi]
+            codes = raw[q][:, i].rearrange("p b t -> p (b t)")[:, lo:hi].bitcast(FP8)
+            return wide, codes
 
-        def widen_half(h):
-            if h >= B:
+        def widen_s(q, i, lo=0, hi=None):
+            if q >= PAIRS:
                 return
-            q = h // 2
-            if h % 2 == 0:
-                new_planes(q)
-            for i in (2 * (h % 2), 2 * (h % 2) + 1):
-                wide = planes[q][:, i].rearrange("p b t -> p (b t)")
-                codes = raw[q][:, i].rearrange("p b t -> p (b t)").bitcast(FP8)
-                if (q == 1 and i % 2) or (q % 4 == 3 and i == 3):
-                    nc.vector.tensor_scalar(out=wide, in0=codes, scalar1=xs[:, i : i + 1], scalar2=None, op0=ALU.mult)
-                else:
-                    nc.scalar.activation(out=wide, in_=codes, func=ACT.Copy, scale=xs[:, i : i + 1])
+            if q not in planes:
+                planes[q] = pln.tile([P, 4, 2, T], BF16, name="planes", align_bytes=64)
+            if hi is None:
+                hi = 2 * T - vector_widens(q).get(i, 0)
+            wide, codes = slot_views(q, i, lo, hi)
+            nc.scalar.activation(out=wide, in_=codes, func=ACT.Copy, scale=xs[:, i : i + 1])
 
-        new_planes(0)
-        for b in (0, 1):
-            for i in range(4):
-                if i < 2:
-                    nc.vector.tensor_scalar(
-                        out=planes[0][:, i, b, :], in0=raw[0][:, i, b, :].bitcast(FP8),
-                        scalar1=xs[:, i : i + 1], scalar2=None, op0=ALU.mult,
-                    )
-                else:
-                    nc.scalar.activation(
-                        out=planes[0][:, i, b, :], in_=raw[0][:, i, b, :].bitcast(FP8),
-                        func=ACT.Copy, scale=xs[:, i : i + 1],
-                    )
-        for h in range(2, AHEAD):
-            widen_half(h)
+        def widen_v(q, i, lo, hi):
+            wide, codes = slot_views(q, i, lo, hi)
+            nc.vector.tensor_scalar(out=wide, in0=codes, scalar1=xs[:, i : i + 1], scalar2=None, op0=ALU.mult)
 
-        w1_words = w1_sb[:].bitcast(F32)
-        w1_t = ps_h.tile([P, 512], F32, name="h_ps")
-        for u in (0, 1):
-            nc.tensor.transpose(w1_t[:, 128 * u : 128 * (u + 1)], w1_words[:, u : 256 : 2], ident[:])
+        def widen_tails(q):
+            for i, cols in vector_widens(q).items():
+                if cols:
+                    widen_v(q, i, 2 * T - cols, 2 * T)
+
         w1_g = keep.tile([P, 512], BF16, name="w1_g", align_bytes=64)
         w1_c = keep.tile([P, 128], U32, name="w1_c", align_bytes=64)
         w1_s = keep.tile([P, 128], U8, name="w1_s", align_bytes=64)
@@ -141,15 +128,19 @@ def tile_temporalaugmentedbilinear_t_kernel(tc, x_bytes, x_scale, w1, g, w, w2, 
         w_c = keep.tile([P, 256], U32, name="w_c", align_bytes=64)
         w_s = keep.tile([P, 256], U8, name="w_s", align_bytes=64)
 
-        g_t = ps_i.tile([P, P], BF16, name="id_ps")
-        nc.tensor.transpose(g_t[:], g_rows[:], ident_b[:])
+        w1_words = w1_sb[:].bitcast(F32)
+        w1_t = ps_h.tile([P, 512], F32, name="h_ps")
+        for u in (0, 1):
+            nc.tensor.transpose(w1_t[:, 128 * u : 128 * (u + 1)], w1_words[:, u : 256 : 2], ident[:])
+        g_t = ps_i.tile([P, 64 * TENSOR_RUNS], BF16, name="id_ps")
+        nc.tensor.transpose(g_t[:, 0:P], g_rows[:], ident_b[:])
 
         def prep_w1_copy():
-            nc.vector.tensor_copy(out=g_sb[:], in_=g_t[:, 0:4])
             nc.vector.tensor_copy(
                 out=w1_g[:].bitcast(F32).rearrange("p (r u) -> p r u", u=2),
                 in_=w1_t[:, 0:256].rearrange("p (u r) -> p r u", u=2),
             )
+            nc.vector.tensor_copy(out=g_sb[:], in_=g_t[:, 0:4])
 
         def prep_w1_quant():
             nc.vector.quantize_mx(out=w1_c[:].bitcast(FP8X4), scales=w1_s[:], in_=w1_g[:])
@@ -166,205 +157,249 @@ def tile_temporalaugmentedbilinear_t_kernel(tc, x_bytes, x_scale, w1, g, w, w2, 
                 out=w_c[:].bitcast(FP8X4), scales=w_s[:], in_=w_g[:].rearrange("p a q j -> p (a q j)")
             )
 
-        lam_lo = keep.tile([P, 1], F32, name="lam_lo")
-        lam_hi = keep.tile([P, 1], F32, name="lam_hi")
+        lam128 = keep.tile([P, 1], F32, name="lam128")
+        near0 = keep.tile([P, 1], F32, name="near0")
         c128 = keep.tile([P, 1], F32, name="c128")
-        oml = keep.tile([P, 1], F32, name="oml")
         rc = keep.tile([P, 1], F32, name="rc")
-        coef = keep.tile([P, 2], F32, name="coef")
-        TINY = 1e-20
+        kneg = keep.tile([P, 1], F32, name="kneg")
+        bias_c = keep.tile([P, Q], F32, name="bias_c")
+        bias_ps = ps_c.tile([P, Q], F32, name="bias_ps")
+        TINY = 1e-16
 
-        def prep_lam():
-            nc.gpsimd.tensor_scalar(out=lam_lo[:], in0=lam_sb[:], scalar1=TINY, scalar2=TINY, op0=ALU.is_lt, op1=ALU.mult)
-            nc.gpsimd.tensor_scalar(out=lam_hi[:], in0=lam_sb[:], scalar1=-TINY, scalar2=None, op0=ALU.is_gt)
-            nc.gpsimd.tensor_tensor(out=lam_lo[:], in0=lam_lo[:], in1=lam_hi[:], op=ALU.mult)
-            nc.gpsimd.tensor_tensor(out=c128[:], in0=lam_lo[:], in1=lam_sb[:], op=ALU.add)
-            nc.gpsimd.tensor_scalar(out=c128[:], in0=c128[:], scalar1=128.0, scalar2=None, op0=ALU.mult)
-            nc.gpsimd.tensor_scalar(out=oml[:], in0=lam_sb[:], scalar1=-1.0, scalar2=1.0, op0=ALU.mult, op1=ALU.add)
-            nc.vector.reciprocal(rc[:], c128[:])
-            nc.gpsimd.tensor_copy(out=coef[:, 0:1], in_=rc[:])
-            nc.gpsimd.tensor_tensor(out=coef[:, 1:2], in0=oml[:], in1=rc[:], op=ALU.mult)
+        lam_steps = [
+            lambda: nc.vector.tensor_scalar(out=lam128[:], in0=lam_sb[:], scalar1=128.0, scalar2=None, op0=ALU.mult),
+            lambda: nc.vector.tensor_scalar(
+                out=near0[:], in0=lam128[:], scalar1=lam128[:], scalar2=TINY * TINY, op0=ALU.mult, op1=ALU.is_lt
+            ),
+            lambda: nc.vector.scalar_tensor_tensor(
+                out=c128[:], in0=near0[:], scalar=2 * TINY, in1=lam128[:], op0=ALU.mult, op1=ALU.add
+            ),
+            lambda: nc.vector.reciprocal(rc[:], c128[:]),
+            lambda: nc.vector.scalar_tensor_tensor(
+                out=kneg[:], in0=lam_sb[:], scalar=1.0, in1=rc[:], op0=ALU.subtract, op1=ALU.mult
+            ),
+            lambda: nc.vector.tensor_scalar(out=bias_c[:], in0=bias_sb[:], scalar1=rc[:], scalar2=None, op0=ALU.mult),
+        ]
 
         grouped, xc, xsc = {}, {}, {}
 
-        def lay(n, part):
-            s = shares(n)
-            a0 = sum(s[:part])
-            a1 = a0 + s[part]
-            src = planes[n // 2][:, :, n % 2, :].rearrange("p i (s j r) -> p s j r i", j=4, r=4)
-            dst = grouped[n][:].rearrange("p j s r i -> p s j r i")
+        def lay(q, r, a0, a1):
+            if (q, r) not in grouped:
+                grouped[q, r] = grp.tile([P, 4, RUNS, 4, 4], BF16, name="grouped%d" % r, align_bytes=64)
+            src = planes[q][:, :, r, :].rearrange("p i (s j r) -> p s j r i", j=4, r=4)
+            dst = grouped[q, r][:].rearrange("p j s r i -> p s j r i")
             return src[:, a0:a1], dst[:, a0:a1]
 
-        def interleave_g(n):
-            if n >= B:
-                return
-            grouped[n] = grp.tile([P, 4, 32, 4, 4], BF16, name="grouped", align_bytes=64)
-            if shares(n)[3]:
-                src, dst = lay(n, 3)
-                nc.gpsimd.tensor_scalar(out=dst, in0=src, scalar1=1.0, scalar2=0.0, op0=ALU.mult, op1=ALU.add)
+        def lay_v(q, r, a0, a1):
+            if a1 > a0:
+                src, dst = (ap.rearrange("p s j r i -> p s j i r") for ap in lay(q, r, a0, a1))
+                nc.vector.tensor_copy(out=dst, in_=src)
 
-        def interleave_v(n):
-            src, dst = (ap.rearrange("p s j r i -> p s j i r") for ap in lay(n, 0))
-            nc.vector.tensor_copy(out=dst, in_=src)
+        def lay_g(q):
+            src, dst = lay(q, 1, RUNS - gpsimd_runs(q), RUNS)
+            nc.gpsimd.tensor_scalar(out=dst, in0=src, scalar1=1.0, scalar2=0.0, op0=ALU.mult, op1=ALU.add)
 
         id_ps = {}
 
-        def interleave_t(n):
-            if n >= B or not shares(n)[2]:
-                return
-            src, dst = lay(n, 2)
-            id_ps[n] = ps_i.tile([P, 256], BF16, name="id_ps")
-            nc.tensor.matmul(
-                id_ps[n][:].rearrange("p (t i) -> p t i", i=4), lhsT=ident_b[:],
-                rhs=src.rearrange("p s j r i -> p (s j r) i"), start=True, stop=True,
-            )
-
-        def interleave_s(n):
-            if n >= B:
-                return
-            if shares(n)[2]:
-                src, dst = lay(n, 2)
-                nc.scalar.copy(
-                    out=dst.rearrange("p s j r i -> p s j (r i)"),
-                    in_=id_ps[n][:].rearrange("p (s j c) -> p s j c", j=4, c=16),
+        def lay_t(q):
+            id_ps[q] = ps_i.tile([P, 64 * TENSOR_RUNS], BF16, name="id_ps")
+            half = TENSOR_RUNS // 2
+            for a0, a1 in ((0, half), (half, TENSOR_RUNS)):
+                src, dst = lay(q, 1, a0, a1)
+                nc.tensor.matmul(
+                    id_ps[q][:, 64 * a0 : 64 * a1].rearrange("p (t i) -> p t i", i=4), lhsT=ident_b[:],
+                    rhs=src.rearrange("p s j r i -> p (s j r) i"), start=True, stop=True,
                 )
-            if shares(n)[1]:
-                src, dst = lay(n, 1)
-                nc.scalar.copy(out=dst, in_=src)
 
-        def quant(n):
-            xc[n] = cod.tile([P, 512], U32, name="xc", align_bytes=64)
-            xsc[n] = cod.tile([P, 512], U8, name="xsc", align_bytes=64)
-            nc.vector.quantize_mx(
-                out=xc[n][:].bitcast(FP8X4), scales=xsc[n][:],
-                in_=grouped[n][:].rearrange("p j s r i -> p (j s r i)"),
+        def lay_s(q):
+            src, dst = lay(q, 1, 0, TENSOR_RUNS)
+            nc.scalar.copy(
+                out=dst.rearrange("p s j r i -> p s j (r i)"),
+                in_=id_ps[q][:].rearrange("p (s j c) -> p s j c", j=4, c=16),
             )
 
         h_ps = {}
 
-        def mm1(n):
-            h_ps[n] = ps_h.tile([P, 512], F32, name="h_ps")
+        def quant(q, r):
+            xc = cod.tile([P, 512], U32, name="xc%d" % r, align_bytes=64)
+            xsc = cod.tile([P, 512], U8, name="xsc%d" % r, align_bytes=64)
+            nc.vector.quantize_mx(
+                out=xc[:].bitcast(FP8X4), scales=xsc[:],
+                in_=grouped[q, r][:].rearrange("p j s r i -> p (j s r i)"),
+            )
+            h_ps[q, r] = ps_h.tile([P, 512], F32, name="h_ps")
             for j in range(4):
                 cols = slice(128 * j, 128 * (j + 1))
                 nc.tensor.matmul_mx(
-                    out=h_ps[n][:, cols],
-                    lhsT=xc[n][:, cols].bitcast(FP8X4), lhsT_scale=xsc[n][:, cols],
+                    out=h_ps[q, r][:, cols],
+                    lhsT=xc[:, cols].bitcast(FP8X4), lhsT_scale=xsc[:, cols],
                     rhs=w1_c[:].bitcast(FP8X4), rhs_scale=w1_s[:],
                     start=True, stop=True,
                 )
 
-        hg, hc, hs = {}, {}, {}
+        hg = {}
 
-        def gain(n):
-            q = n // 2
-            if n % 2 == 0:
+        def gain(q, r):
+            if r == 0:
                 hg[q] = hp.tile([P, 2, PF, 4], BF16, name="hg", align_bytes=64)
             nc.vector.tensor_tensor(
-                out=hg[q][:, n % 2],
-                in0=h_ps[n][:].rearrange("p (j f) -> p f j", j=4),
+                out=hg[q][:, r],
+                in0=h_ps[q, r][:].rearrange("p (j f) -> p f j", j=4),
                 in1=g_sb[:].unsqueeze(1).to_broadcast([P, PF, 4]),
                 op=ALU.mult,
             )
 
-        def hquant(q):
-            hc[q] = hp.tile([P, 2 * PF], U32, name="hc", align_bytes=64)
-            hs[q] = hp.tile([P, 2 * PF], U8, name="hs", align_bytes=64)
+        ue, mn, sm, kn, rs, ex = {}, {}, {}, {}, {}, {}
+
+        def hquant(q, rows=(0, 1)):
+            n = len(rows)
+            hc = hp.tile([P, n * PF], U32, name="hc", align_bytes=64)
+            hs = hp.tile([P, n * PF], U8, name="hs", align_bytes=64)
             nc.vector.quantize_mx(
-                out=hc[q][:].bitcast(FP8X4), scales=hs[q][:], in_=hg[q][:].rearrange("p b f j -> p (b f j)")
+                out=hc[:].bitcast(FP8X4), scales=hs[:],
+                in_=hg[q][:, rows[0] : rows[0] + n].rearrange("p b f j -> p (b f j)"),
             )
-
-        ue = {}
-
-        def mm2(q):
-            ue[q] = ps_ue.tile([P, 2, 2, Q], F32, name="ue")
-            for r in (0, 1):
-                rows = slice(PF * r, PF * (r + 1))
+            ue[q, rows] = ps_ue.tile([P, n, 2, Q], F32, name="ue")
+            for k in range(n):
+                cols = slice(PF * k, PF * (k + 1))
                 nc.tensor.matmul_mx(
-                    out=ue[q][:, r].rearrange("p a q -> p (a q)"),
-                    lhsT=hc[q][:, rows].bitcast(FP8X4), lhsT_scale=hs[q][:, rows],
+                    out=ue[q, rows][:, k].rearrange("p a q -> p (a q)"),
+                    lhsT=hc[:, cols].bitcast(FP8X4), lhsT_scale=hs[:, cols],
                     rhs=w_c[:].bitcast(FP8X4), rhs_scale=w_s[:],
                     start=True, stop=True,
                 )
 
-        mn, sm, fac, cc, ex = {}, {}, {}, {}, {}
+        def row_max(q, rows=(0, 1)):
+            mn[q, rows] = ep.tile([P, len(rows)], F32, name="mn")
+            nc.vector.tensor_reduce(out=mn[q, rows][:], in_=ue[q, rows][:, :, 1], axis=AX.X, op=ALU.min)
 
-        def row_max(q):
-            mn[q] = ep.tile([P, 2], F32, name="mn")
-            nc.vector.tensor_reduce(out=mn[q][:], in_=ue[q][:, :, 1], axis=AX.X, op=ALU.min)
-
-        def exps(q):
-            sm[q] = ep.tile([P, 2], F32, name="sm")
-            ex[q] = ep.tile([P, 2, Q], F32, name="ex")
-            for r in (0, 1):
+        def exps(q, rows=(0, 1)):
+            sm[q, rows] = ep.tile([P, len(rows)], F32, name="sm")
+            ex[q, rows] = ep.tile([P, len(rows), Q], F32, name="ex")
+            for k in range(len(rows)):
                 nc.scalar.activation(
-                    out=ex[q][:, r], in_=ue[q][:, r, 1], func=ACT.Exp,
-                    bias=mn[q][:, r : r + 1], scale=-1.0, accum_out=sm[q][:, r : r + 1],
+                    out=ex[q, rows][:, k], in_=ue[q, rows][:, k, 1], func=ACT.Exp,
+                    bias=mn[q, rows][:, k : k + 1], scale=-1.0, accum_out=sm[q, rows][:, k : k + 1],
                 )
 
-        def factors(q):
-            fac[q] = ep.tile([P, 2, 2], F32, name="fac")
-            nc.gpsimd.tensor_tensor(
-                out=fac[q][:], in0=sm[q][:].unsqueeze(1).to_broadcast([P, 2, 2]),
-                in1=coef[:].unsqueeze(2).to_broadcast([P, 2, 2]), op=ALU.mult,
-            )
+        def offsets(q, rows=(0, 1)):
+            kn[q, rows] = ep.tile([P, len(rows)], F32, name="kn")
+            nc.scalar.activation(out=kn[q, rows][:], in_=sm[q, rows][:], func=ACT.Copy, scale=kneg[:])
 
-        def invert(q):
-            cc[q] = ep.tile([P, 2], F32, name="cc")
-            nc.vector.reciprocal(cc[q][:], fac[q][:, 0])
+        def invert(q, rows=(0, 1)):
+            rs[q, rows] = ep.tile([P, len(rows)], F32, name="rs")
+            nc.vector.reciprocal(rs[q, rows][:], sm[q, rows][:])
 
-        def weigh(q):
-            for r in (0, 1):
+        def weigh(q, rows=(0, 1)):
+            for k in range(len(rows)):
                 nc.vector.scalar_tensor_tensor(
-                    out=ex[q][:, r], in0=ex[q][:, r], scalar=fac[q][:, 1, r : r + 1], in1=ue[q][:, r, 0],
-                    op0=ALU.add, op1=ALU.mult,
+                    out=ex[q, rows][:, k], in0=ex[q, rows][:, k], scalar=kn[q, rows][:, k : k + 1],
+                    in1=ue[q, rows][:, k, 0], op0=ALU.subtract, op1=ALU.mult,
                 )
 
-        def mix(q):
-            for r in (0, 1):
+        def mix(q, rows=(0, 1)):
+            for k in range(len(rows)):
                 nc.vector.scalar_tensor_tensor(
-                    out=ex[q][:, r], in0=ex[q][:, r], scalar=cc[q][:, r : r + 1], in1=bias_sb[:],
-                    op0=ALU.mult, op1=ALU.add,
+                    out=ex[q, rows][:, k], in0=ex[q, rows][:, k], scalar=rs[q, rows][:, k : k + 1],
+                    in1=bias_ps[:], op0=ALU.mult, op1=ALU.add,
                 )
 
-        def finish(q):
-            o = ep.tile([P, 2, Q], F32, name="o")
-            nc.scalar.activation(out=o[:], in_=ex[q][:], func=ACT.Tanh)
-            nc.sync.dma_start(out=out[2 * q : 2 * q + 2].rearrange("b p q -> p b q"), in_=o[:])
+        def finish(q, rows=(0, 1)):
+            o = ep.tile([P, len(rows), Q], F32, name="o")
+            nc.scalar.activation(out=o[:], in_=ex[q, rows][:], func=ACT.Tanh, scale=c128[:])
+            b0 = 2 * q + rows[0]
+            nc.sync.dma_start(out=out[b0 : b0 + len(rows)].rearrange("b p q -> p b q"), in_=o[:])
 
-        def at(stage, lag, n):
-            if 0 <= n - lag < B and (n - lag) % 2 == 0:
-                stage((n - lag) // 2)
+        def when(q, stage, *args):
+            if 0 <= q < PAIRS:
+                stage(q, *args)
 
-        interleave_g(0)
-        interleave_g(1)
-        for n in range(B + 9):
-            load(n + LOAD_AHEAD)
-            if 0 <= n - 1 < B:
-                quant(n - 1)
-                mm1(n - 1)
-            if n < B:
-                interleave_v(n)
-            if n == 0:
-                prep_w1_copy()
-                prep_w1_quant()
-                prep_lam()
-            if n == 2:
+        planes[0] = pln.tile([P, 4, 2, T], BF16, name="planes", align_bytes=64)
+        for r in (0, 1):
+            widen_s(0, 3, r * T, (r + 1) * T)
+            for i in range(3):
+                widen_v(0, i, r * T, (r + 1) * T)
+        for i in range(4):
+            widen_s(1, i)
+        lay_v(0, 0, 0, RUNS)
+        prep_w1_copy()
+        lay_v(0, 1, 0, RUNS)
+        prep_w1_quant()
+        lay_t(1)
+
+        last = PAIRS - 1
+        for q in range(last):
+            load(q + LOAD_AHEAD)
+            widen_s(q + 2, 0)
+            by_scalar = SCALAR_LAST_RUNS if q + 1 == last else 0
+            if by_scalar:
+                src, dst = lay(last, 0, 0, by_scalar)
+                nc.scalar.copy(out=dst, in_=src)
+            when(q - 1, hquant)
+            when(q - 2, invert)
+            when(q - 3, finish)
+            lay_s(q + 1)
+            quant(q, 0)
+            if q == 0:
                 prep_w_copy()
-            if n == 3:
+            if q < 2:
+                lam_steps[3 * q]()
+            quant(q, 1)
+            if q == 0:
                 prep_w_quant()
-            interleave_g(n + 2)
-            at(factors, 7, n)
-            interleave_t(n + 2)
-            interleave_s(n + 1)
-            if 0 <= n - 2 < B:
-                gain(n - 2)
-            at(invert, 8, n)
-            at(weigh, 8, n)
-            at(row_max, 5, n)
-            at(mix, 9, n)
-            if n + AHEAD < B:
-                widen_half(n + AHEAD)
-            at(exps, 6, n)
-            at(hquant, 4, n)
-            at(mm2, 4, n)
-            at(finish, 10, n)
+            if q < 2:
+                lam_steps[3 * q + 1]()
+            widen_s(q + 2, 1)
+            widen_s(q + 2, 2)
+            lay_v(q + 1, 1, TENSOR_RUNS, RUNS - gpsimd_runs(q + 1))
+            if q < 2:
+                lam_steps[3 * q + 2]()
+            widen_tails(q + 1)
+            lay_g(q + 1)
+            lay_v(q + 1, 0, by_scalar, RUNS)
+            when(q - 1, row_max)
+            gain(q, 0)
+            when(q - 1, exps)
+            when(q - 2, weigh)
+            gain(q, 1)
+            when(q - 2, mix)
+            if q == 1:
+                nc.tensor.matmul(bias_ps[:], lhsT=ident[:], rhs=bias_c[:], start=True, stop=True)
+            widen_s(q + 2, 3)
+            when(q - 1, offsets)
+            when(q + 2, lay_t)
+
+        first, second = (0,), (1,)
+        hquant(last - 1)
+        invert(last - 2)
+        finish(last - 3)
+        quant(last, 0)
+        quant(last, 1)
+        row_max(last - 1)
+        exps(last - 1)
+        weigh(last - 2)
+        gain(last, 0)
+        offsets(last - 1)
+        mix(last - 2)
+        finish(last - 2)
+        hquant(last, first)
+        gain(last, 1)
+        invert(last - 1)
+        weigh(last - 1)
+        hquant(last, second)
+        row_max(last, first)
+        exps(last, first)
+        mix(last - 1)
+        offsets(last, first)
+        row_max(last, second)
+        exps(last, second)
+        invert(last, first)
+        weigh(last, first)
+        offsets(last, second)
+        finish(last - 1)
+        invert(last, second)
+        mix(last, first)
+        weigh(last, second)
+        finish(last, first)
+        mix(last, second)
+        finish(last, second)

@@ -25,12 +25,12 @@ SCALAR_LAST_RUNS = 24
 
 
 def gpsimd_runs(q):
-    return {0: 0, 1: 10, 2: 14, PAIRS - 1: 20}.get(q, 22)
+    return {0: 0, 1: 8, 2: 12, PAIRS - 1: 12}.get(q, 14)
 
 
 def vector_widens(q):
     room = 16 * gpsimd_runs(q)
-    return {2: min(0, room), 3: min(320, room)}
+    return {2: min(0, room), 3: min(128, room)}
 
 
 def tile_temporalaugmentedbilinear_t_kernel(tc, x_bytes, x_scale, w1, g, w, w2, lam, bias, out):
@@ -338,7 +338,6 @@ def tile_temporalaugmentedbilinear_t_kernel(tc, x_bytes, x_scale, w1, g, w, w2, 
             when(q - 1, hquant)
             when(q - 2, invert)
             when(q - 3, finish)
-            lay_s(q + 1)
             quant(q, 0)
             if q == 0:
                 prep_w_copy()
@@ -350,6 +349,7 @@ def tile_temporalaugmentedbilinear_t_kernel(tc, x_bytes, x_scale, w1, g, w, w2, 
             if q < 2:
                 lam_steps[3 * q + 1]()
             widen_s(q + 2, 1)
+            lay_s(q + 1)
             widen_s(q + 2, 2)
             lay_v(q + 1, 1, TENSOR_RUNS, RUNS - gpsimd_runs(q + 1))
             if q < 2:
@@ -360,8 +360,8 @@ def tile_temporalaugmentedbilinear_t_kernel(tc, x_bytes, x_scale, w1, g, w, w2, 
             when(q - 1, row_max)
             gain(q, 0)
             when(q - 1, exps)
-            when(q - 2, weigh)
             gain(q, 1)
+            when(q - 2, weigh)
             when(q - 2, mix)
             if q == 1:
                 nc.tensor.matmul(bias_ps[:], lhsT=ident[:], rhs=bias_c[:], start=True, stop=True)

@@ -25,12 +25,12 @@ SCALAR_LAST_RUNS = 24
 
 
 def gpsimd_runs(q):
-    return {0: 0, 1: 8, 2: 12, PAIRS - 1: 12}.get(q, 14)
+    return {0: 0, 1: 8, 2: 12, PAIRS - 1: 12}.get(q, 20)
 
 
 def vector_widens(q):
     room = 16 * gpsimd_runs(q)
-    return {2: min(0, room), 3: min(128, room)}
+    return {2: min(0, room), 3: min(256, room)}
 
 
 def tile_temporalaugmentedbilinear_t_kernel(tc, x_bytes, x_scale, w1, g, w, w2, lam, bias, out):

@@ -30,7 +30,7 @@ def gpsimd_runs(q):
 
 def vector_widens(q):
     room = 16 * gpsimd_runs(q)
-    return {2: min(0, room), 3: min(256, room)}
+    return {2: min(0, room), 3: min(64, room)}
 
 
 def tile_temporalaugmentedbilinear_t_kernel(tc, x_bytes, x_scale, w1, g, w, w2, lam, bias, out):
@@ -181,22 +181,32 @@ def tile_temporalaugmentedbilinear_t_kernel(tc, x_bytes, x_scale, w1, g, w, w2, 
             lambda: nc.vector.tensor_scalar(out=bias_c[:], in0=bias_sb[:], scalar1=rc[:], scalar2=None, op0=ALU.mult),
         ]
 
-        grouped, xc, xsc = {}, {}, {}
+        grouped = {}
+        split = (0, PAIRS - 1)
 
-        def lay(q, r, a0, a1):
-            if (q, r) not in grouped:
-                grouped[q, r] = grp.tile([P, 4, RUNS, 4, 4], BF16, name="grouped%d" % r, align_bytes=64)
-            src = planes[q][:, :, r, :].rearrange("p i (s j r) -> p s j r i", j=4, r=4)
-            dst = grouped[q, r][:].rearrange("p j s r i -> p s j r i")
-            return src[:, a0:a1], dst[:, a0:a1]
+        def lay(q, a0, a1):
+            if q not in grouped:
+                grouped[q] = grp.tile([P, 4096], BF16, name="grouped", align_bytes=64)
+            src = planes[q][:].rearrange("p i b (s j r) -> p (b s) j r i", j=4, r=4)[:, a0:a1]
+            if q in split:
+                b = a0 // RUNS
+                half = grouped[q][:, 2048 * b : 2048 * (b + 1)]
+                dst = half.rearrange("p (j s r i) -> p s j r i", j=4, r=4, i=4)[:, a0 - RUNS * b : a1 - RUNS * b]
+            else:
+                dst = grouped[q][:].rearrange("p (j u r i) -> p u j r i", j=4, r=4, i=4)[:, a0:a1]
+            return src, dst
 
-        def lay_v(q, r, a0, a1):
-            if a1 > a0:
-                src, dst = (ap.rearrange("p s j r i -> p s j i r") for ap in lay(q, r, a0, a1))
+        def lay_v(q, a0, a1):
+            cuts = [a0, RUNS, a1] if q in split and a0 < RUNS < a1 else [a0, a1]
+            for lo, hi in zip(cuts, cuts[1:]):
+                src, dst = (ap.rearrange("p s j r i -> p s j i r") for ap in lay(q, lo, hi))
                 nc.vector.tensor_copy(out=dst, in_=src)
 
+        def first_tensor_run(q):
+            return 2 * RUNS - gpsimd_runs(q) - TENSOR_RUNS
+
         def lay_g(q):
-            src, dst = lay(q, 1, RUNS - gpsimd_runs(q), RUNS)
+            src, dst = lay(q, 2 * RUNS - gpsimd_runs(q), 2 * RUNS)
             nc.gpsimd.tensor_scalar(out=dst, in0=src, scalar1=1.0, scalar2=0.0, op0=ALU.mult, op1=ALU.add)
 
         id_ps = {}
@@ -205,14 +215,14 @@ def tile_temporalaugmentedbilinear_t_kernel(tc, x_bytes, x_scale, w1, g, w, w2, 
             id_ps[q] = ps_i.tile([P, 64 * TENSOR_RUNS], BF16, name="id_ps")
             half = TENSOR_RUNS // 2
             for a0, a1 in ((0, half), (half, TENSOR_RUNS)):
-                src, dst = lay(q, 1, a0, a1)
+                src, dst = lay(q, first_tensor_run(q) + a0, first_tensor_run(q) + a1)
                 nc.tensor.matmul(
                     id_ps[q][:, 64 * a0 : 64 * a1].rearrange("p (t i) -> p t i", i=4), lhsT=ident_b[:],
                     rhs=src.rearrange("p s j r i -> p (s j r) i"), start=True, stop=True,
                 )
 
         def lay_s(q):
-            src, dst = lay(q, 1, 0, TENSOR_RUNS)
+            src, dst = lay(q, first_tensor_run(q), first_tensor_run(q) + TENSOR_RUNS)
             nc.scalar.copy(
                 out=dst.rearrange("p s j r i -> p s j (r i)"),
                 in_=id_ps[q][:].rearrange("p (s j c) -> p s j c", j=4, c=16),
@@ -220,22 +230,23 @@ def tile_temporalaugmentedbilinear_t_kernel(tc, x_bytes, x_scale, w1, g, w, w2, 
 
         h_ps = {}
 
-        def quant(q, r):
-            xc = cod.tile([P, 512], U32, name="xc%d" % r, align_bytes=64)
-            xsc = cod.tile([P, 512], U8, name="xsc%d" % r, align_bytes=64)
+        def quant(q, rows=(0, 1)):
+            n = len(rows)
+            xc = cod.tile([P, 512 * n], U32, name="xc", align_bytes=64)
+            xsc = cod.tile([P, 512 * n], U8, name="xsc", align_bytes=64)
             nc.vector.quantize_mx(
-                out=xc[:].bitcast(FP8X4), scales=xsc[:],
-                in_=grouped[q, r][:].rearrange("p j s r i -> p (j s r i)"),
+                out=xc[:].bitcast(FP8X4), scales=xsc[:], in_=grouped[q][:, 2048 * rows[0] : 2048 * (rows[0] + n)]
             )
-            h_ps[q, r] = ps_h.tile([P, 512], F32, name="h_ps")
-            for j in range(4):
-                cols = slice(128 * j, 128 * (j + 1))
-                nc.tensor.matmul_mx(
-                    out=h_ps[q, r][:, cols],
-                    lhsT=xc[:, cols].bitcast(FP8X4), lhsT_scale=xsc[:, cols],
-                    rhs=w1_c[:].bitcast(FP8X4), rhs_scale=w1_s[:],
-                    start=True, stop=True,
-                )
+            for k, r in enumerate(rows):
+                h_ps[q, r] = ps_h.tile([P, 512], F32, name="h_ps")
+                for j in range(4):
+                    cols = slice(128 * (n * j + k), 128 * (n * j + k + 1))
+                    nc.tensor.matmul_mx(
+                        out=h_ps[q, r][:, 128 * j : 128 * (j + 1)],
+                        lhsT=xc[:, cols].bitcast(FP8X4), lhsT_scale=xsc[:, cols],
+                        rhs=w1_c[:].bitcast(FP8X4), rhs_scale=w1_s[:],
+                        start=True, stop=True,
+                    )
 
         hg = {}
 
@@ -321,9 +332,9 @@ def tile_temporalaugmentedbilinear_t_kernel(tc, x_bytes, x_scale, w1, g, w, w2, 
                 widen_v(0, i, r * T, (r + 1) * T)
         for i in range(4):
             widen_s(1, i)
-        lay_v(0, 0, 0, RUNS)
+        lay_v(0, 0, RUNS)
         prep_w1_copy()
-        lay_v(0, 1, 0, RUNS)
+        lay_v(0, RUNS, 2 * RUNS)
         prep_w1_quant()
         lay_t(1)
 
@@ -331,32 +342,34 @@ def tile_temporalaugmentedbilinear_t_kernel(tc, x_bytes, x_scale, w1, g, w, w2, 
         for q in range(last):
             load(q + LOAD_AHEAD)
             widen_s(q + 2, 0)
+            when(q - 2, offsets)
             by_scalar = SCALAR_LAST_RUNS if q + 1 == last else 0
             if by_scalar:
-                src, dst = lay(last, 0, 0, by_scalar)
+                src, dst = lay(last, 0, by_scalar)
                 nc.scalar.copy(out=dst, in_=src)
             when(q - 1, hquant)
-            when(q - 2, invert)
-            when(q - 3, finish)
-            quant(q, 0)
-            if q == 0:
-                prep_w_copy()
             if q < 2:
                 lam_steps[3 * q]()
-            quant(q, 1)
+            when(q - 3, finish)
             if q == 0:
+                quant(0, (0,))
+                prep_w_copy()
+                quant(0, (1,))
                 prep_w_quant()
+            else:
+                quant(q)
             if q < 2:
                 lam_steps[3 * q + 1]()
             widen_s(q + 2, 1)
             lay_s(q + 1)
             widen_s(q + 2, 2)
-            lay_v(q + 1, 1, TENSOR_RUNS, RUNS - gpsimd_runs(q + 1))
+            widen_s(q + 2, 3)
+            when(q - 2, invert)
+            widen_tails(q + 1)
             if q < 2:
                 lam_steps[3 * q + 2]()
-            widen_tails(q + 1)
             lay_g(q + 1)
-            lay_v(q + 1, 0, by_scalar, RUNS)
+            lay_v(q + 1, by_scalar, first_tensor_run(q + 1))
             when(q - 1, row_max)
             gain(q, 0)
             when(q - 1, exps)
@@ -365,16 +378,15 @@ def tile_temporalaugmentedbilinear_t_kernel(tc, x_bytes, x_scale, w1, g, w, w2, 
             when(q - 2, mix)
             if q == 1:
                 nc.tensor.matmul(bias_ps[:], lhsT=ident[:], rhs=bias_c[:], start=True, stop=True)
-            widen_s(q + 2, 3)
-            when(q - 1, offsets)
             when(q + 2, lay_t)
 
         first, second = (0,), (1,)
+        offsets(last - 2)
         hquant(last - 1)
         invert(last - 2)
         finish(last - 3)
-        quant(last, 0)
-        quant(last, 1)
+        quant(last, first)
+        quant(last, second)
         row_max(last - 1)
         exps(last - 1)
         weigh(last - 2)

@@ -25,7 +25,11 @@ SCALAR_LAST_RUNS = 24
 
 
 def gpsimd_runs(q):
-    return {0: 0, 1: 8, 2: 12, PAIRS - 1: 12}.get(q, 20)
+    return {0: 0, 1: 12, 2: 16, PAIRS - 1: 16}.get(q, 24)
+
+
+def scalar_empties(q):
+    return False
 
 
 def vector_widens(q):
@@ -221,9 +225,9 @@ def tile_temporalaugmentedbilinear_t_kernel(tc, x_bytes, x_scale, w1, g, w, w2, 
                     rhs=src.rearrange("p s j r i -> p (s j r) i"), start=True, stop=True,
                 )
 
-        def lay_s(q):
+        def lay_out(q, copy):
             src, dst = lay(q, first_tensor_run(q), first_tensor_run(q) + TENSOR_RUNS)
-            nc.scalar.copy(
+            copy(
                 out=dst.rearrange("p s j r i -> p s j (r i)"),
                 in_=id_ps[q][:].rearrange("p (s j c) -> p s j c", j=4, c=16),
             )
@@ -361,7 +365,8 @@ def tile_temporalaugmentedbilinear_t_kernel(tc, x_bytes, x_scale, w1, g, w, w2, 
             if q < 2:
                 lam_steps[3 * q + 1]()
             widen_s(q + 2, 1)
-            lay_s(q + 1)
+            if scalar_empties(q + 1):
+                lay_out(q + 1, nc.scalar.copy)
             widen_s(q + 2, 2)
             widen_s(q + 2, 3)
             when(q - 2, invert)
@@ -371,6 +376,8 @@ def tile_temporalaugmentedbilinear_t_kernel(tc, x_bytes, x_scale, w1, g, w, w2, 
             lay_g(q + 1)
             lay_v(q + 1, by_scalar, first_tensor_run(q + 1))
             when(q - 1, row_max)
+            if not scalar_empties(q + 1):
+                lay_out(q + 1, nc.vector.tensor_copy)
             gain(q, 0)
             when(q - 1, exps)
             gain(q, 1)

@@ -17,54 +17,84 @@ ACT = mybir.ActivationFunctionType
 AX = mybir.AxisListType
 
 P = 128
-PAIRS = B // 2
 RUNS = 32
-TENSOR_RUNS = 10
-LOAD_AHEAD = 4
-SCALAR_LAST_RUNS = 24
+UNITS = (2,) * 16
+LAST = len(UNITS) - 1
+TENSOR_RUNS = 5
+RELEASE_COLUMNS = 160
+SCALAR_LAST_RUNS = 26
 
 
-def gpsimd_runs(q):
-    return {0: 0, 1: 12, 2: 16, PAIRS - 1: 16}.get(q, 24)
+def size(u):
+    return UNITS[u] if 0 <= u <= LAST else 0
 
 
-def scalar_empties(q):
-    return False
+def tensor_runs(u):
+    return TENSOR_RUNS * size(u) if 0 < u < LAST else 0
 
 
-def vector_widens(q):
-    room = 16 * gpsimd_runs(q)
-    return {2: min(0, room), 3: min(64, room)}
+def scalar_runs(u):
+    if u == LAST:
+        return SCALAR_LAST_RUNS
+    if size(u + 1) < size(u):
+        return 0
+    return 0 if u > 2 else 0
+
+
+def vector_columns(u):
+    return {}.get(u, 0)
+
+
+def scalar_empties(u):
+    return u == LAST
+
+
+def gpsimd_runs(u):
+    return {0: 0, 1: 16, 2: 22, LAST: 20}.get(u, 26)
+
+
+def cast_runs(u):
+    return {0: 0, 1: 0, LAST: 0}.get(u, 0)
 
 
 def tile_temporalaugmentedbilinear_t_kernel(tc, x_bytes, x_scale, w1, g, w, w2, lam, bias, out):
     nc = tc.nc
+    first_batch = [sum(UNITS[:u]) for u in range(len(UNITS))]
     with ExitStack() as ctx:
         keep = ctx.enter_context(tc.tile_pool(name="keep", bufs=1))
-        raws = ctx.enter_context(tc.tile_pool(name="raws", bufs=LOAD_AHEAD + 1))
+        raws = ctx.enter_context(tc.tile_pool(name="raws", bufs=4))
         pln = ctx.enter_context(tc.tile_pool(name="pln", bufs=3))
         grp = ctx.enter_context(tc.tile_pool(name="grp", bufs=2))
         cod = ctx.enter_context(tc.tile_pool(name="cod", bufs=2))
         hp = ctx.enter_context(tc.tile_pool(name="hp", bufs=2))
         ep = ctx.enter_context(tc.tile_pool(name="ep", bufs=4))
-        ps_h = ctx.enter_context(tc.psum_pool(name="ps_h", bufs=2))
-        ps_ue = ctx.enter_context(tc.psum_pool(name="ps_ue", bufs=3))
+        ps_h = ctx.enter_context(tc.psum_pool(name="ps_h", bufs=3))
+        ps_ue = ctx.enter_context(tc.psum_pool(name="ps_ue", bufs=2))
         ps_i = ctx.enter_context(tc.psum_pool(name="ps_i", bufs=2))
         ps_c = ctx.enter_context(tc.psum_pool(name="ps_c", bufs=1))
         ctx.enter_context(tc.manual_schedule())
 
-        raw = {}
+        raw, raw_cast = {}, {}
 
-        def load(q):
-            if q >= PAIRS:
-                return
-            raw[q] = raws.tile([P, 4, 2, T], U8, name="raw", align_bytes=64)
-            for r in (0, 1):
-                load_batch(q, r)
+        def width(u):
+            return 2 * T - 16 * cast_runs(u)
 
-        def load_batch(q, r, slots=slice(0, 4)):
-            rows = x_bytes[2 * q + r].rearrange("(p i) t -> p i t", i=4)
-            nc.sync.dma_start(out=raw[q][:, slots, r, :], in_=rows[:, slots])
+        def load_batch(u, r, slots=slice(0, 4)):
+            if u not in raw:
+                raw[u] = raws.tile([P, 4, width(u)], U8, name="raw", align_bytes=64)
+            rows = x_bytes[first_batch[u] + r].rearrange("(p i) t -> p i t", i=4)
+            cast = 16 * cast_runs(u)
+            if r == 0 and cast:
+                raw_cast[u] = raws.tile([P, 4, cast], U8, name="raw_cast", align_bytes=64)
+                nc.sync.dma_start(out=raw_cast[u][:], in_=rows[:, :, 0:cast])
+            if r == 0:
+                nc.sync.dma_start(out=raw[u][:, slots, 0 : T - cast], in_=rows[:, slots, cast:T])
+            else:
+                nc.sync.dma_start(out=raw[u][:, slots, T - cast :], in_=rows[:, slots])
+
+        def load(u):
+            for r in range(size(u)):
+                load_batch(u, r)
 
         xs = keep.tile([P, 4], F32, name="xs")
         w1_sb = keep.tile([P, D], BF16, name="w1_sb", align_bytes=64)
@@ -75,24 +105,22 @@ def tile_temporalaugmentedbilinear_t_kernel(tc, x_bytes, x_scale, w1, g, w, w2, 
         g_rows = keep.tile([P, P], BF16, name="g_rows", align_bytes=64)
 
         nc.scalar.dma_start(out=xs[:], in_=x_scale.rearrange("o (p i) z -> p (o i z)", i=4))
-        raw[0] = raws.tile([P, 4, 2, T], U8, name="raw", align_bytes=64)
         load_batch(0, 0, slice(0, 2))
         load_batch(0, 0, slice(2, 4))
         load_batch(0, 1)
         nc.sync.dma_start(out=w1_sb[:], in_=w1)
         load(1)
         nc.gpsimd.memset(g_rows[:], 0.0)
-        nc.scalar.dma_start(
+        nc.sync.dma_start(
             out=g_rows[0:4, :].rearrange("j (s r) -> j s r", r=4), in_=g.rearrange("(s j r) -> j s r", j=4, r=4)
         )
-        nc.scalar.dma_start(out=lam_sb[:], in_=lam.rearrange("(p o) -> p o", o=1))
-        load(2)
-        nc.sync.dma_start(out=bias_sb[:], in_=bias)
         for k, wt in enumerate((w2, w)):
             rows = wt.rearrange("(s j r) q -> r s j q", j=4, r=4)
             for r in range(4):
                 nc.sync.dma_start(out=w_sb[r:P:4, k], in_=rows[r])
-        load(3)
+        nc.sync.dma_start(out=lam_sb[:], in_=lam.rearrange("(p o) -> p o", o=1))
+        load(2)
+        nc.sync.dma_start(out=bias_sb[:], in_=bias)
 
         ident = keep.tile([P, P], F32, name="ident")
         make_identity(nc, ident[:])
@@ -101,29 +129,33 @@ def tile_temporalaugmentedbilinear_t_kernel(tc, x_bytes, x_scale, w1, g, w, w2, 
 
         planes = {}
 
-        def slot_views(q, i, lo, hi):
-            wide = planes[q][:, i].rearrange("p b t -> p (b t)")[:, lo:hi]
-            codes = raw[q][:, i].rearrange("p b t -> p (b t)")[:, lo:hi].bitcast(FP8)
-            return wide, codes
+        def slot_views(u, i, lo, hi):
+            if u not in planes:
+                planes[u] = pln.tile([P, 4, width(u)], BF16, name="planes", align_bytes=64)
+            codes = raw[u][:, i, lo:hi].bitcast(FP8)
+            return planes[u][:, i, lo:hi], codes
 
-        def widen_s(q, i, lo=0, hi=None):
-            if q >= PAIRS:
+        def widen_s(u, i, lo=0, hi=None):
+            if u > LAST:
                 return
-            if q not in planes:
-                planes[q] = pln.tile([P, 4, 2, T], BF16, name="planes", align_bytes=64)
             if hi is None:
-                hi = 2 * T - vector_widens(q).get(i, 0)
-            wide, codes = slot_views(q, i, lo, hi)
+                hi = width(u) - (RELEASE_COLUMNS if i == 3 else 0)
+            wide, codes = slot_views(u, i, lo, hi)
             nc.scalar.activation(out=wide, in_=codes, func=ACT.Copy, scale=xs[:, i : i + 1])
 
-        def widen_v(q, i, lo, hi):
-            wide, codes = slot_views(q, i, lo, hi)
-            nc.vector.tensor_scalar(out=wide, in0=codes, scalar1=xs[:, i : i + 1], scalar2=None, op0=ALU.mult)
+        values = {}
 
-        def widen_tails(q):
-            for i, cols in vector_widens(q).items():
-                if cols:
-                    widen_v(q, i, 2 * T - cols, 2 * T)
+        def cast_s(u):
+            if u <= LAST and cast_runs(u):
+                values[u] = pln.tile([P, 4, 16 * cast_runs(u)], BF16, name="values", align_bytes=64)
+                nc.scalar.copy(
+                    out=values[u][:].rearrange("p i t -> p (i t)"),
+                    in_=raw_cast[u][:].rearrange("p i t -> p (i t)").bitcast(FP8),
+                )
+
+        def widen_v(u, i, lo, hi):
+            wide, codes = slot_views(u, i, lo, hi)
+            nc.vector.tensor_scalar(out=wide, in0=codes, scalar1=xs[:, i : i + 1], scalar2=None, op0=ALU.mult)
 
         w1_g = keep.tile([P, 512], BF16, name="w1_g", align_bytes=64)
         w1_c = keep.tile([P, 128], U32, name="w1_c", align_bytes=64)
@@ -136,15 +168,14 @@ def tile_temporalaugmentedbilinear_t_kernel(tc, x_bytes, x_scale, w1, g, w, w2, 
         w1_t = ps_h.tile([P, 512], F32, name="h_ps")
         for u in (0, 1):
             nc.tensor.transpose(w1_t[:, 128 * u : 128 * (u + 1)], w1_words[:, u : 256 : 2], ident[:])
-        g_t = ps_i.tile([P, 64 * TENSOR_RUNS], BF16, name="id_ps")
-        nc.tensor.transpose(g_t[:, 0:P], g_rows[:], ident_b[:])
+        g_t = ps_i.tile([P, P], BF16, name="id_ps")
+        nc.tensor.transpose(g_t[:], g_rows[:], ident_b[:])
 
         def prep_w1_copy():
             nc.vector.tensor_copy(
                 out=w1_g[:].bitcast(F32).rearrange("p (r u) -> p r u", u=2),
                 in_=w1_t[:, 0:256].rearrange("p (u r) -> p r u", u=2),
             )
-            nc.vector.tensor_copy(out=g_sb[:], in_=g_t[:, 0:4])
 
         def prep_w1_quant():
             nc.vector.quantize_mx(out=w1_c[:].bitcast(FP8X4), scales=w1_s[:], in_=w1_g[:])
@@ -167,7 +198,9 @@ def tile_temporalaugmentedbilinear_t_kernel(tc, x_bytes, x_scale, w1, g, w, w2, 
         rc = keep.tile([P, 1], F32, name="rc")
         kneg = keep.tile([P, 1], F32, name="kneg")
         bias_c = keep.tile([P, Q], F32, name="bias_c")
-        bias_ps = ps_c.tile([P, Q], F32, name="bias_ps")
+        consts = ps_c.tile([P, Q + 4], F32, name="consts")
+        bias_ps = consts[:, 0:Q]
+        xs_ps = consts[:, Q : Q + 4]
         TINY = 1e-16
 
         lam_steps = [
@@ -186,239 +219,291 @@ def tile_temporalaugmentedbilinear_t_kernel(tc, x_bytes, x_scale, w1, g, w, w2, 
         ]
 
         grouped = {}
-        split = (0, PAIRS - 1)
+        by_batch = (0, LAST)
 
-        def lay(q, a0, a1):
-            if q not in grouped:
-                grouped[q] = grp.tile([P, 4096], BF16, name="grouped", align_bytes=64)
-            src = planes[q][:].rearrange("p i b (s j r) -> p (b s) j r i", j=4, r=4)[:, a0:a1]
-            if q in split:
-                b = a0 // RUNS
-                half = grouped[q][:, 2048 * b : 2048 * (b + 1)]
-                dst = half.rearrange("p (j s r i) -> p s j r i", j=4, r=4, i=4)[:, a0 - RUNS * b : a1 - RUNS * b]
+        def lay(u, a0, a1):
+            if u not in grouped:
+                grouped[u] = grp.tile([P, 2048 * size(u)], BF16, name="grouped", align_bytes=64)
+            f = cast_runs(u)
+            if a0 < f:
+                src = values[u][:].rearrange("p i (s j r) -> p s j r i", j=4, r=4)[:, a0:a1]
             else:
-                dst = grouped[q][:].rearrange("p (j u r i) -> p u j r i", j=4, r=4, i=4)[:, a0:a1]
-            return src, dst
+                src = planes[u][:].rearrange("p i (s j r) -> p s j r i", j=4, r=4)[:, a0 - f : a1 - f]
+            if u in by_batch:
+                b = a0 // RUNS
+                part = grouped[u][:, 2048 * b : 2048 * (b + 1)]
+                return src, part.rearrange("p (j s r i) -> p s j r i", j=4, r=4, i=4)[:, a0 - RUNS * b : a1 - RUNS * b]
+            return src, grouped[u][:].rearrange("p (j s r i) -> p s j r i", j=4, r=4, i=4)[:, a0:a1]
 
-        def lay_v(q, a0, a1):
-            cuts = [a0, RUNS, a1] if q in split and a0 < RUNS < a1 else [a0, a1]
+        def lay_v(u, a0, a1):
+            if a1 <= a0:
+                return
+            cuts = [a0, RUNS, a1] if u in by_batch and a0 < RUNS < a1 else [a0, a1]
             for lo, hi in zip(cuts, cuts[1:]):
-                src, dst = (ap.rearrange("p s j r i -> p s j i r") for ap in lay(q, lo, hi))
+                src, dst = (ap.rearrange("p s j r i -> p s j i r") for ap in lay(u, lo, hi))
                 nc.vector.tensor_copy(out=dst, in_=src)
 
-        def first_tensor_run(q):
-            return 2 * RUNS - gpsimd_runs(q) - TENSOR_RUNS
+        def lay_scaled(u):
+            if cast_runs(u):
+                src, dst = lay(u, 0, cast_runs(u))
+                nc.vector.tensor_tensor(
+                    out=dst.rearrange("p s j r i -> p s j (r i)"), in0=src.rearrange("p s j r i -> p (s j r) i"),
+                    in1=xs_ps.unsqueeze(1).to_broadcast([P, 16 * cast_runs(u), 4]), op=ALU.mult,
+                )
 
-        def lay_g(q):
-            src, dst = lay(q, 2 * RUNS - gpsimd_runs(q), 2 * RUNS)
+        def lay_s(u):
+            if scalar_runs(u):
+                src, dst = lay(u, cast_runs(u), cast_runs(u) + scalar_runs(u))
+                nc.scalar.copy(out=dst, in_=src)
+
+        def first_tensor_run(u):
+            return RUNS * size(u) - gpsimd_runs(u) - tensor_runs(u)
+
+        def lay_g(u):
+            src, dst = lay(u, RUNS * size(u) - gpsimd_runs(u), RUNS * size(u))
             nc.gpsimd.tensor_scalar(out=dst, in0=src, scalar1=1.0, scalar2=0.0, op0=ALU.mult, op1=ALU.add)
 
         id_ps = {}
 
-        def lay_t(q):
-            id_ps[q] = ps_i.tile([P, 64 * TENSOR_RUNS], BF16, name="id_ps")
-            half = TENSOR_RUNS // 2
-            for a0, a1 in ((0, half), (half, TENSOR_RUNS)):
-                src, dst = lay(q, first_tensor_run(q) + a0, first_tensor_run(q) + a1)
-                nc.tensor.matmul(
-                    id_ps[q][:, 64 * a0 : 64 * a1].rearrange("p (t i) -> p t i", i=4), lhsT=ident_b[:],
-                    rhs=src.rearrange("p s j r i -> p (s j r) i"), start=True, stop=True,
-                )
-
-        def lay_out(q, copy):
-            src, dst = lay(q, first_tensor_run(q), first_tensor_run(q) + TENSOR_RUNS)
-            copy(
-                out=dst.rearrange("p s j r i -> p s j (r i)"),
-                in_=id_ps[q][:].rearrange("p (s j c) -> p s j c", j=4, c=16),
-            )
-
-        h_ps = {}
-
-        def quant(q, rows=(0, 1)):
-            n = len(rows)
-            xc = cod.tile([P, 512 * n], U32, name="xc", align_bytes=64)
-            xsc = cod.tile([P, 512 * n], U8, name="xsc", align_bytes=64)
-            nc.vector.quantize_mx(
-                out=xc[:].bitcast(FP8X4), scales=xsc[:], in_=grouped[q][:, 2048 * rows[0] : 2048 * (rows[0] + n)]
-            )
-            for k, r in enumerate(rows):
-                h_ps[q, r] = ps_h.tile([P, 512], F32, name="h_ps")
-                for j in range(4):
-                    cols = slice(128 * (n * j + k), 128 * (n * j + k + 1))
-                    nc.tensor.matmul_mx(
-                        out=h_ps[q, r][:, 128 * j : 128 * (j + 1)],
-                        lhsT=xc[:, cols].bitcast(FP8X4), lhsT_scale=xsc[:, cols],
-                        rhs=w1_c[:].bitcast(FP8X4), rhs_scale=w1_s[:],
-                        start=True, stop=True,
+        def lay_t(u):
+            for h in range(size(u) // 2):
+                id_ps[u, h] = ps_i.tile([P, 2, 64 * TENSOR_RUNS], BF16, name="id_ps")
+                for k in (0, 1):
+                    a0 = first_tensor_run(u) + TENSOR_RUNS * (2 * h + k)
+                    src, dst = lay(u, a0, a0 + TENSOR_RUNS)
+                    nc.tensor.matmul(
+                        id_ps[u, h][:, k].rearrange("p (t i) -> p t i", i=4), lhsT=ident_b[:],
+                        rhs=src.rearrange("p s j r i -> p (s j r) i"), start=True, stop=True,
                     )
 
-        hg = {}
+        def lay_out(u, h, copy):
+            if h < size(u) // 2:
+                a0 = first_tensor_run(u) + 2 * TENSOR_RUNS * h
+                src, dst = lay(u, a0, a0 + 2 * TENSOR_RUNS)
+                copy(
+                    out=dst.rearrange("p s j r i -> p s j (r i)"),
+                    in_=id_ps[u, h][:].rearrange("p k (s j c) -> p (k s) j c", j=4, c=16),
+                )
 
-        def gain(q, r):
+        xc, xsc, h_ps, hg = {}, {}, {}, {}
+
+        def quant(u, lo, hi):
+            if u not in xc:
+                xc[u] = cod.tile([P, 512 * size(u)], U32, name="xc", align_bytes=64)
+                xsc[u] = cod.tile([P, 512 * size(u)], U8, name="xsc", align_bytes=64)
+            nc.vector.quantize_mx(
+                out=xc[u][:, lo // 4 : hi // 4].bitcast(FP8X4), scales=xsc[u][:, lo // 4 : hi // 4],
+                in_=grouped[u][:, lo:hi],
+            )
+
+        def features(u, r):
+            h_ps[u, r] = ps_h.tile([P, 512], F32, name="h_ps")
+            for j in range(4):
+                tile = 4 * r + j if u in by_batch else size(u) * j + r
+                cols = slice(128 * tile, 128 * (tile + 1))
+                nc.tensor.matmul_mx(
+                    out=h_ps[u, r][:, 128 * j : 128 * (j + 1)],
+                    lhsT=xc[u][:, cols].bitcast(FP8X4), lhsT_scale=xsc[u][:, cols],
+                    rhs=w1_c[:].bitcast(FP8X4), rhs_scale=w1_s[:],
+                    start=True, stop=True,
+                )
+
+        def gain(u, r):
+            if r >= size(u):
+                return
             if r == 0:
-                hg[q] = hp.tile([P, 2, PF, 4], BF16, name="hg", align_bytes=64)
+                hg[u] = hp.tile([P, size(u), PF, 4], BF16, name="hg", align_bytes=64)
             nc.vector.tensor_tensor(
-                out=hg[q][:, r],
-                in0=h_ps[q, r][:].rearrange("p (j f) -> p f j", j=4),
+                out=hg[u][:, r],
+                in0=h_ps[u, r][:].rearrange("p (j f) -> p f j", j=4),
                 in1=g_sb[:].unsqueeze(1).to_broadcast([P, PF, 4]),
                 op=ALU.mult,
             )
 
         ue, mn, sm, kn, rs, ex = {}, {}, {}, {}, {}, {}
 
-        def hquant(q, rows=(0, 1)):
-            n = len(rows)
+        def banks(n):
+            return [(k, min(2, n - k)) for k in range(0, n, 2)]
+
+        def hquant(part):
+            u, r0, n = part
             hc = hp.tile([P, n * PF], U32, name="hc", align_bytes=64)
             hs = hp.tile([P, n * PF], U8, name="hs", align_bytes=64)
             nc.vector.quantize_mx(
-                out=hc[:].bitcast(FP8X4), scales=hs[:],
-                in_=hg[q][:, rows[0] : rows[0] + n].rearrange("p b f j -> p (b f j)"),
+                out=hc[:].bitcast(FP8X4), scales=hs[:], in_=hg[u][:, r0 : r0 + n].rearrange("p b f j -> p (b f j)")
             )
-            ue[q, rows] = ps_ue.tile([P, n, 2, Q], F32, name="ue")
-            for k in range(n):
-                cols = slice(PF * k, PF * (k + 1))
-                nc.tensor.matmul_mx(
-                    out=ue[q, rows][:, k].rearrange("p a q -> p (a q)"),
-                    lhsT=hc[:, cols].bitcast(FP8X4), lhsT_scale=hs[:, cols],
-                    rhs=w_c[:].bitcast(FP8X4), rhs_scale=w_s[:],
-                    start=True, stop=True,
-                )
+            for k0, m in banks(n):
+                if u == LAST:
+                    bank = ps_h.tile([P, m, 2, Q], F32, name="h_ps")
+                else:
+                    bank = ps_ue.tile([P, m, 2, Q], F32, name="ue")
+                ue[part, k0] = bank
+                for k in range(m):
+                    cols = slice(PF * (k0 + k), PF * (k0 + k + 1))
+                    nc.tensor.matmul_mx(
+                        out=bank[:, k].rearrange("p a q -> p (a q)"),
+                        lhsT=hc[:, cols].bitcast(FP8X4), lhsT_scale=hs[:, cols],
+                        rhs=w_c[:].bitcast(FP8X4), rhs_scale=w_s[:],
+                        start=True, stop=True,
+                    )
 
-        def row_max(q, rows=(0, 1)):
-            mn[q, rows] = ep.tile([P, len(rows)], F32, name="mn")
-            nc.vector.tensor_reduce(out=mn[q, rows][:], in_=ue[q, rows][:, :, 1], axis=AX.X, op=ALU.min)
+        def row_max(part):
+            mn[part] = ep.tile([P, part[2]], F32, name="mn")
+            for k0, m in banks(part[2]):
+                nc.vector.tensor_reduce(out=mn[part][:, k0 : k0 + m], in_=ue[part, k0][:, :, 1], axis=AX.X, op=ALU.min)
 
-        def exps(q, rows=(0, 1)):
-            sm[q, rows] = ep.tile([P, len(rows)], F32, name="sm")
-            ex[q, rows] = ep.tile([P, len(rows), Q], F32, name="ex")
-            for k in range(len(rows)):
+        def exps(part):
+            sm[part] = ep.tile([P, part[2]], F32, name="sm")
+            ex[part] = ep.tile([P, part[2], Q], F32, name="ex")
+            for k in range(part[2]):
                 nc.scalar.activation(
-                    out=ex[q, rows][:, k], in_=ue[q, rows][:, k, 1], func=ACT.Exp,
-                    bias=mn[q, rows][:, k : k + 1], scale=-1.0, accum_out=sm[q, rows][:, k : k + 1],
+                    out=ex[part][:, k], in_=ue[part, k - k % 2][:, k % 2, 1], func=ACT.Exp,
+                    bias=mn[part][:, k : k + 1], scale=-1.0, accum_out=sm[part][:, k : k + 1],
                 )
 
-        def offsets(q, rows=(0, 1)):
-            kn[q, rows] = ep.tile([P, len(rows)], F32, name="kn")
-            nc.scalar.activation(out=kn[q, rows][:], in_=sm[q, rows][:], func=ACT.Copy, scale=kneg[:])
+        def offsets(part):
+            kn[part] = ep.tile([P, part[2]], F32, name="kn")
+            nc.scalar.activation(out=kn[part][:], in_=sm[part][:], func=ACT.Copy, scale=kneg[:])
 
-        def invert(q, rows=(0, 1)):
-            rs[q, rows] = ep.tile([P, len(rows)], F32, name="rs")
-            nc.vector.reciprocal(rs[q, rows][:], sm[q, rows][:])
+        def invert(part):
+            rs[part] = ep.tile([P, part[2]], F32, name="rs")
+            nc.vector.reciprocal(rs[part][:], sm[part][:])
 
-        def weigh(q, rows=(0, 1)):
-            for k in range(len(rows)):
+        def weigh(part):
+            for k in range(part[2]):
                 nc.vector.scalar_tensor_tensor(
-                    out=ex[q, rows][:, k], in0=ex[q, rows][:, k], scalar=kn[q, rows][:, k : k + 1],
-                    in1=ue[q, rows][:, k, 0], op0=ALU.subtract, op1=ALU.mult,
+                    out=ex[part][:, k], in0=ex[part][:, k], scalar=kn[part][:, k : k + 1],
+                    in1=ue[part, k - k % 2][:, k % 2, 0], op0=ALU.subtract, op1=ALU.mult,
                 )
 
-        def mix(q, rows=(0, 1)):
-            for k in range(len(rows)):
+        def mix(part):
+            for k in range(part[2]):
                 nc.vector.scalar_tensor_tensor(
-                    out=ex[q, rows][:, k], in0=ex[q, rows][:, k], scalar=rs[q, rows][:, k : k + 1],
-                    in1=bias_ps[:], op0=ALU.mult, op1=ALU.add,
+                    out=ex[part][:, k], in0=ex[part][:, k], scalar=rs[part][:, k : k + 1],
+                    in1=bias_ps, op0=ALU.mult, op1=ALU.add,
                 )
 
-        def finish(q, rows=(0, 1)):
-            o = ep.tile([P, len(rows), Q], F32, name="o")
-            nc.scalar.activation(out=o[:], in_=ex[q, rows][:], func=ACT.Tanh, scale=c128[:])
-            b0 = 2 * q + rows[0]
-            nc.sync.dma_start(out=out[b0 : b0 + len(rows)].rearrange("b p q -> p b q"), in_=o[:])
+        def finish(part):
+            u, r0, n = part
+            o = ep.tile([P, n, Q], F32, name="o")
+            nc.scalar.activation(out=o[:], in_=ex[part][:], func=ACT.Tanh, scale=c128[:])
+            b0 = first_batch[u] + r0
+            nc.sync.dma_start(out=out[b0 : b0 + n].rearrange("b p q -> p b q"), in_=o[:])
 
-        def when(q, stage, *args):
-            if 0 <= q < PAIRS:
-                stage(q, *args)
+        def whole(u, stage):
+            if u >= 0:
+                stage((u, 0, size(u)))
 
-        planes[0] = pln.tile([P, 4, 2, T], BF16, name="planes", align_bytes=64)
         for r in (0, 1):
-            widen_s(0, 3, r * T, (r + 1) * T)
-            for i in range(3):
-                widen_v(0, i, r * T, (r + 1) * T)
+            for i in range(4):
+                widen = widen_v if i < 3 - r else widen_s
+                widen(0, i, r * T, (r + 1) * T)
         for i in range(4):
-            widen_s(1, i)
+            widen_s(1, i, 0, width(1) - T)
+        for i in range(4):
+            widen_s(1, i, width(1) - T)
         lay_v(0, 0, RUNS)
         prep_w1_copy()
         lay_v(0, RUNS, 2 * RUNS)
         prep_w1_quant()
-        lay_t(1)
 
-        last = PAIRS - 1
-        for q in range(last):
-            load(q + LOAD_AHEAD)
-            widen_s(q + 2, 0)
-            when(q - 2, offsets)
-            by_scalar = SCALAR_LAST_RUNS if q + 1 == last else 0
-            if by_scalar:
-                src, dst = lay(last, 0, by_scalar)
-                nc.scalar.copy(out=dst, in_=src)
-            when(q - 1, hquant)
-            if q < 2:
-                lam_steps[3 * q]()
-            when(q - 3, finish)
-            if q == 0:
-                quant(0, (0,))
-                prep_w_copy()
-                quant(0, (1,))
+        for u in range(LAST):
+            n = size(u)
+            load(u + 3)
+            widen_s(u + 2, 0)
+            lay_s(u + 1)
+            if vector_columns(u + 1):
+                widen_v(u + 1, 2, 0, vector_columns(u + 1))
+            if u == 1:
+                lam_steps[2]()
                 prep_w_quant()
+            whole(u - 1, hquant)
+            if 0 < u < LAST - 1:
+                lay_t(u + 1)
+            if u == 1:
+                lam_steps[3]()
+            if u == 0:
+                quant(0, 0, 2048)
+                quant(0, 2048, 4096)
             else:
-                quant(q)
-            if q < 2:
-                lam_steps[3 * q + 1]()
-            widen_s(q + 2, 1)
-            if scalar_empties(q + 1):
-                lay_out(q + 1, nc.scalar.copy)
-            widen_s(q + 2, 2)
-            widen_s(q + 2, 3)
-            when(q - 2, invert)
-            widen_tails(q + 1)
-            if q < 2:
-                lam_steps[3 * q + 2]()
-            lay_g(q + 1)
-            lay_v(q + 1, by_scalar, first_tensor_run(q + 1))
-            when(q - 1, row_max)
-            if not scalar_empties(q + 1):
-                lay_out(q + 1, nc.vector.tensor_copy)
-            gain(q, 0)
-            when(q - 1, exps)
-            gain(q, 1)
-            when(q - 2, weigh)
-            when(q - 2, mix)
-            if q == 1:
-                nc.tensor.matmul(bias_ps[:], lhsT=ident[:], rhs=bias_c[:], start=True, stop=True)
-            when(q + 2, lay_t)
+                for lo in range(0, 2048 * n, 4096):
+                    quant(u, lo, lo + 4096)
+            for r in range(min(n, 3)):
+                features(u, r)
+            if u == 0:
+                nc.vector.tensor_copy(out=g_sb[:], in_=g_t[:, 0:4])
+            if u == 0:
+                lay_t(u + 1)
+            if u < 2:
+                lam_steps[4 * u]()
+            widen_s(u + 2, 1)
+            if vector_columns(u + 2) < size(u + 2) * T:
+                widen_s(u + 2, 2, vector_columns(u + 2))
+            whole(u - 2, invert)
+            if u == 0:
+                prep_w_copy()
+            widen_v(u + 1, 3, width(u + 1) - RELEASE_COLUMNS, width(u + 1))
+            if u < 2:
+                lam_steps[4 * u + 1]()
+            lay_g(u + 1)
+            lay_v(u + 1, cast_runs(u + 1) + scalar_runs(u + 1), first_tensor_run(u + 1) if u + 1 < LAST else RUNS)
+            lay_scaled(u + 1)
+            if u == 1:
+                nc.tensor.matmul(bias_ps, lhsT=ident[:], rhs=bias_c[:], start=True, stop=True)
+            whole(u - 1, row_max)
+            whole(u - 1, exps)
+            if u + 1 == LAST:
+                src, dst = lay(LAST, RUNS, first_tensor_run(LAST))
+                nc.scalar.copy(out=dst, in_=src)
+            whole(u - 2, mix)
+            gain(u, 0)
+            if n == 4:
+                features(u, 3)
+            whole(u - 2, finish)
+            whole(u - 1, offsets)
+            if not scalar_empties(u + 1):
+                lay_out(u + 1, 0, nc.vector.tensor_copy)
+            gain(u, 1)
+            gain(u, 2)
+            if not scalar_empties(u + 1):
+                lay_out(u + 1, 1, nc.vector.tensor_copy)
+            gain(u, 3)
+            if u < LAST - 1:
+                whole(u - 1, weigh)
+            widen_s(u + 2, 3)
 
-        first, second = (0,), (1,)
-        offsets(last - 2)
-        hquant(last - 1)
-        invert(last - 2)
-        finish(last - 3)
-        quant(last, first)
-        quant(last, second)
-        row_max(last - 1)
-        exps(last - 1)
-        weigh(last - 2)
-        gain(last, 0)
-        offsets(last - 1)
-        mix(last - 2)
-        finish(last - 2)
-        hquant(last, first)
-        gain(last, 1)
-        invert(last - 1)
-        weigh(last - 1)
-        hquant(last, second)
-        row_max(last, first)
-        exps(last, first)
-        mix(last - 1)
-        offsets(last, first)
-        row_max(last, second)
-        exps(last, second)
-        invert(last, first)
-        weigh(last, first)
-        offsets(last, second)
-        finish(last - 1)
-        invert(last, second)
-        mix(last, first)
-        weigh(last, second)
-        finish(last, first)
-        mix(last, second)
-        finish(last, second)
+        first, second = (LAST, 0, 1), (LAST, 1, 1)
+        whole(LAST - 1, hquant)
+        quant(LAST, 0, 2048)
+        features(LAST, 0)
+        whole(LAST - 2, invert)
+        quant(LAST, 2048, 4096)
+        features(LAST, 1)
+        whole(LAST - 1, row_max)
+        whole(LAST - 1, exps)
+        whole(LAST - 2, weigh)
+        gain(LAST, 0)
+        whole(LAST - 1, offsets)
+        gain(LAST, 1)
+        hquant(first)
+        whole(LAST - 2, mix)
+        whole(LAST - 2, finish)
+        hquant(second)
+        whole(LAST - 1, invert)
+        whole(LAST - 1, weigh)
+        row_max(first)
+        exps(first)
+        row_max(second)
+        exps(second)
+        offsets(first)
+        whole(LAST - 1, mix)
+        offsets(second)
+        invert(first)
+        weigh(first)
+        invert(second)
+        whole(LAST - 1, finish)
+        weigh(second)
+        mix(first)
+        mix(second)
+        finish(first)
+        finish(second)

@@ -407,45 +407,46 @@ def tile_temporalaugmentedbilinear_t_kernel(tc, x_bytes, x_scale, w1, g, w, w2, 
         lay_v(0, RUNS, 2 * RUNS)
         prep_w1_quant()
 
+        def release(u):
+            widen_v(u, 3, width(u) - RELEASE_COLUMNS, width(u))
+            lay_g(u)
+
         for u in range(LAST):
             n = size(u)
+            early = cast_runs(u + 1) > 0
             load(u + 3)
             widen_s(u + 2, 0)
             lay_s(u + 1)
-            if vector_columns(u + 1):
-                widen_v(u + 1, 2, 0, vector_columns(u + 1))
             if u == 1:
                 lam_steps[2]()
                 prep_w_quant()
-            whole(u - 1, hquant)
+                lam_steps[3]()
             if 0 < u < LAST - 1:
                 lay_t(u + 1)
+            whole(u - 1, hquant)
             if u == 1:
-                lam_steps[3]()
+                lam_steps[4]()
+                lam_steps[5]()
+            whole(u - 2, invert)
+            if early:
+                release(u + 1)
             if u == 0:
                 quant(0, 0, 2048)
                 quant(0, 2048, 4096)
             else:
-                for lo in range(0, 2048 * n, 4096):
-                    quant(u, lo, lo + 4096)
-            for r in range(min(n, 3)):
-                features(u, r)
+                quant(u, 0, 4096)
+            features(u, 0)
+            features(u, 1)
             if u == 0:
                 nc.vector.tensor_copy(out=g_sb[:], in_=g_t[:, 0:4])
-            if u == 0:
-                lay_t(u + 1)
-            if u < 2:
-                lam_steps[4 * u]()
-            widen_s(u + 2, 1)
-            if vector_columns(u + 2) < size(u + 2) * T:
-                widen_s(u + 2, 2, vector_columns(u + 2))
-            whole(u - 2, invert)
-            if u == 0:
+                lay_t(1)
+                lam_steps[0]()
                 prep_w_copy()
-            widen_v(u + 1, 3, width(u + 1) - RELEASE_COLUMNS, width(u + 1))
-            if u < 2:
-                lam_steps[4 * u + 1]()
-            lay_g(u + 1)
+                lam_steps[1]()
+            widen_s(u + 2, 1)
+            widen_s(u + 2, 2)
+            if not early:
+                release(u + 1)
             lay_v(u + 1, cast_runs(u + 1) + scalar_runs(u + 1), first_tensor_run(u + 1) if u + 1 < LAST else RUNS)
             lay_scaled(u + 1)
             if u == 1:
@@ -456,13 +457,15 @@ def tile_temporalaugmentedbilinear_t_kernel(tc, x_bytes, x_scale, w1, g, w, w2, 
                 src, dst = lay(LAST, RUNS, first_tensor_run(LAST))
                 nc.scalar.copy(out=dst, in_=src)
             whole(u - 2, mix)
+            if not scalar_empties(u + 1) and u > 0:
+                lay_out(u + 1, 0, nc.vector.tensor_copy)
             gain(u, 0)
+            if u == 0:
+                lay_out(u + 1, 0, nc.vector.tensor_copy)
             if n == 4:
                 features(u, 3)
             whole(u - 2, finish)
             whole(u - 1, offsets)
-            if not scalar_empties(u + 1):
-                lay_out(u + 1, 0, nc.vector.tensor_copy)
             gain(u, 1)
             gain(u, 2)
             if not scalar_empties(u + 1):

@@ -22,7 +22,7 @@ UNITS = (2,) * 16
 LAST = len(UNITS) - 1
 TENSOR_RUNS = 5
 RELEASE_COLUMNS = 160
-SCALAR_LAST_RUNS = 26
+SCALAR_LAST_RUNS = 22
 
 
 def size(u):
@@ -50,7 +50,11 @@ def scalar_empties(u):
 
 
 def gpsimd_runs(u):
-    return {0: 0, 1: 16, 2: 22, LAST: 20}.get(u, 26)
+    return {0: 0, 1: 14, 2: 20, LAST: 18}.get(u, 24)
+
+
+def release_columns(u):
+    return {1: 160, 2: 160}.get(u, RELEASE_COLUMNS)
 
 
 def cast_runs(u):
@@ -105,11 +109,13 @@ def tile_temporalaugmentedbilinear_t_kernel(tc, x_bytes, x_scale, w1, g, w, w2, 
         g_rows = keep.tile([P, P], BF16, name="g_rows", align_bytes=64)
 
         nc.scalar.dma_start(out=xs[:], in_=x_scale.rearrange("o (p i) z -> p (o i z)", i=4))
+        nc.scalar.dma_start(out=lam_sb[:], in_=lam.rearrange("(p o) -> p o", o=1))
         load_batch(0, 0, slice(0, 2))
         load_batch(0, 0, slice(2, 4))
         load_batch(0, 1)
         nc.sync.dma_start(out=w1_sb[:], in_=w1)
         load(1)
+        load(2)
         nc.gpsimd.memset(g_rows[:], 0.0)
         nc.sync.dma_start(
             out=g_rows[0:4, :].rearrange("j (s r) -> j s r", r=4), in_=g.rearrange("(s j r) -> j s r", j=4, r=4)
@@ -118,8 +124,6 @@ def tile_temporalaugmentedbilinear_t_kernel(tc, x_bytes, x_scale, w1, g, w, w2, 
             rows = wt.rearrange("(s j r) q -> r s j q", j=4, r=4)
             for r in range(4):
                 nc.sync.dma_start(out=w_sb[r:P:4, k], in_=rows[r])
-        nc.sync.dma_start(out=lam_sb[:], in_=lam.rearrange("(p o) -> p o", o=1))
-        load(2)
         nc.sync.dma_start(out=bias_sb[:], in_=bias)
 
         ident = keep.tile([P, P], F32, name="ident")
@@ -139,7 +143,7 @@ def tile_temporalaugmentedbilinear_t_kernel(tc, x_bytes, x_scale, w1, g, w, w2, 
             if u > LAST:
                 return
             if hi is None:
-                hi = width(u) - (RELEASE_COLUMNS if i == 3 else 0)
+                hi = width(u) - (release_columns(u) if i == 3 else 0)
             wide, codes = slot_views(u, i, lo, hi)
             nc.scalar.activation(out=wide, in_=codes, func=ACT.Copy, scale=xs[:, i : i + 1])
 
@@ -398,17 +402,22 @@ def tile_temporalaugmentedbilinear_t_kernel(tc, x_bytes, x_scale, w1, g, w, w2, 
             for i in range(4):
                 widen = widen_v if i < 3 - r else widen_s
                 widen(0, i, r * T, (r + 1) * T)
+            lam_steps[r]()
         for i in range(4):
             widen_s(1, i, 0, width(1) - T)
-        for i in range(4):
+        for i in range(1, 4):
             widen_s(1, i, width(1) - T)
         lay_v(0, 0, RUNS)
+        lam_steps[2]()
         prep_w1_copy()
         lay_v(0, RUNS, 2 * RUNS)
+        lam_steps[3]()
         prep_w1_quant()
+        for i in range(1):
+            widen_v(1, i, T, 2 * T)
 
         def release(u):
-            widen_v(u, 3, width(u) - RELEASE_COLUMNS, width(u))
+            widen_v(u, 3, width(u) - release_columns(u), width(u))
             lay_g(u)
 
         for u in range(LAST):
@@ -418,15 +427,13 @@ def tile_temporalaugmentedbilinear_t_kernel(tc, x_bytes, x_scale, w1, g, w, w2, 
             widen_s(u + 2, 0)
             lay_s(u + 1)
             if u == 1:
-                lam_steps[2]()
-                prep_w_quant()
-                lam_steps[3]()
+                prep_w_copy()
             if 0 < u < LAST - 1:
                 lay_t(u + 1)
-            whole(u - 1, hquant)
             if u == 1:
-                lam_steps[4]()
                 lam_steps[5]()
+                prep_w_quant()
+            whole(u - 1, hquant)
             whole(u - 2, invert)
             if early:
                 release(u + 1)
@@ -438,11 +445,9 @@ def tile_temporalaugmentedbilinear_t_kernel(tc, x_bytes, x_scale, w1, g, w, w2, 
             features(u, 0)
             features(u, 1)
             if u == 0:
-                nc.vector.tensor_copy(out=g_sb[:], in_=g_t[:, 0:4])
                 lay_t(1)
-                lam_steps[0]()
-                prep_w_copy()
-                lam_steps[1]()
+                lam_steps[4]()
+                nc.vector.tensor_copy(out=g_sb[:], in_=g_t[:, 0:4])
             widen_s(u + 2, 1)
             widen_s(u + 2, 2)
             if not early:

@@ -17,88 +17,47 @@ ACT = mybir.ActivationFunctionType
 AX = mybir.AxisListType
 
 P = 128
-RUNS = 32
-UNITS = (2,) * 16
-LAST = len(UNITS) - 1
+LAST = B // 2 - 1
+RUNS = T // 16
+BATCH_COLUMNS = 4 * T
 TENSOR_RUNS = 5
-RELEASE_COLUMNS = 160
+RELEASE_COLUMNS = 96
 SCALAR_LAST_RUNS = 22
+TINY = 1e-16
 
 
-def size(u):
-    return UNITS[u] if 0 <= u <= LAST else 0
-
-
-def tensor_runs(u):
-    return TENSOR_RUNS * size(u) if 0 < u < LAST else 0
-
-
-def scalar_runs(u):
-    if u == LAST:
-        return SCALAR_LAST_RUNS
-    if size(u + 1) < size(u):
-        return 0
-    return 0 if u > 2 else 0
-
-
-def vector_columns(u):
-    return {}.get(u, 0)
-
-
-def scalar_empties(u):
-    return u == LAST
-
-
-def gpsimd_runs(u):
-    return {0: 0, 1: 14, 2: 20, LAST: 18}.get(u, 24)
-
-
-def release_columns(u):
-    return {1: 160, 2: 160}.get(u, RELEASE_COLUMNS)
-
-
-def cast_runs(u):
-    return {0: 0, 1: 0, LAST: 0}.get(u, 0)
+def gpsimd_runs(pair):
+    return {1: 14, 2: 18, LAST: 18}.get(pair, 24)
 
 
 def tile_temporalaugmentedbilinear_t_kernel(tc, x_bytes, x_scale, w1, g, w, w2, lam, bias, out):
     nc = tc.nc
-    first_batch = [sum(UNITS[:u]) for u in range(len(UNITS))]
     with ExitStack() as ctx:
         keep = ctx.enter_context(tc.tile_pool(name="keep", bufs=1))
-        raws = ctx.enter_context(tc.tile_pool(name="raws", bufs=4))
-        pln = ctx.enter_context(tc.tile_pool(name="pln", bufs=3))
-        grp = ctx.enter_context(tc.tile_pool(name="grp", bufs=2))
-        cod = ctx.enter_context(tc.tile_pool(name="cod", bufs=2))
-        hp = ctx.enter_context(tc.tile_pool(name="hp", bufs=2))
-        ep = ctx.enter_context(tc.tile_pool(name="ep", bufs=4))
-        ps_h = ctx.enter_context(tc.psum_pool(name="ps_h", bufs=3))
-        ps_ue = ctx.enter_context(tc.psum_pool(name="ps_ue", bufs=2))
-        ps_i = ctx.enter_context(tc.psum_pool(name="ps_i", bufs=2))
-        ps_c = ctx.enter_context(tc.psum_pool(name="ps_c", bufs=1))
+        raw_pool = ctx.enter_context(tc.tile_pool(name="raw_pool", bufs=4))
+        wide_pool = ctx.enter_context(tc.tile_pool(name="wide_pool", bufs=3))
+        laid_pool = ctx.enter_context(tc.tile_pool(name="laid_pool", bufs=2))
+        code_pool = ctx.enter_context(tc.tile_pool(name="code_pool", bufs=2))
+        h_pool = ctx.enter_context(tc.tile_pool(name="h_pool", bufs=2))
+        tail_pool = ctx.enter_context(tc.tile_pool(name="tail_pool", bufs=4))
+        ps_h = ctx.enter_context(tc.psum_pool(name="ps_h", bufs=2))
+        ps_ue = ctx.enter_context(tc.psum_pool(name="ps_ue", bufs=3))
+        ps_laid = ctx.enter_context(tc.psum_pool(name="ps_laid", bufs=2))
+        ps_bias = ctx.enter_context(tc.psum_pool(name="ps_bias", bufs=1))
         ctx.enter_context(tc.manual_schedule())
 
-        raw, raw_cast = {}, {}
+        raw = {}
 
-        def width(u):
-            return 2 * T - 16 * cast_runs(u)
+        def load_batch(pair, b, slots=slice(0, 4)):
+            if pair not in raw:
+                raw[pair] = raw_pool.tile([P, 4, 2 * T], U8, name="raw", align_bytes=64)
+            rows = x_bytes[2 * pair + b].rearrange("(p i) t -> p i t", i=4)
+            nc.sync.dma_start(out=raw[pair][:, slots, b * T : (b + 1) * T], in_=rows[:, slots])
 
-        def load_batch(u, r, slots=slice(0, 4)):
-            if u not in raw:
-                raw[u] = raws.tile([P, 4, width(u)], U8, name="raw", align_bytes=64)
-            rows = x_bytes[first_batch[u] + r].rearrange("(p i) t -> p i t", i=4)
-            cast = 16 * cast_runs(u)
-            if r == 0 and cast:
-                raw_cast[u] = raws.tile([P, 4, cast], U8, name="raw_cast", align_bytes=64)
-                nc.sync.dma_start(out=raw_cast[u][:], in_=rows[:, :, 0:cast])
-            if r == 0:
-                nc.sync.dma_start(out=raw[u][:, slots, 0 : T - cast], in_=rows[:, slots, cast:T])
-            else:
-                nc.sync.dma_start(out=raw[u][:, slots, T - cast :], in_=rows[:, slots])
-
-        def load(u):
-            for r in range(size(u)):
-                load_batch(u, r)
+        def load(pair):
+            if pair <= LAST:
+                load_batch(pair, 0)
+                load_batch(pair, 1)
 
         xs = keep.tile([P, 4], F32, name="xs")
         w1_sb = keep.tile([P, D], BF16, name="w1_sb", align_bytes=64)
@@ -120,8 +79,8 @@ def tile_temporalaugmentedbilinear_t_kernel(tc, x_bytes, x_scale, w1, g, w, w2, 
         nc.sync.dma_start(
             out=g_rows[0:4, :].rearrange("j (s r) -> j s r", r=4), in_=g.rearrange("(s j r) -> j s r", j=4, r=4)
         )
-        for k, wt in enumerate((w2, w)):
-            rows = wt.rearrange("(s j r) q -> r s j q", j=4, r=4)
+        for k, weight in enumerate((w2, w)):
+            rows = weight.rearrange("(s j r) q -> r s j q", j=4, r=4)
             for r in range(4):
                 nc.sync.dma_start(out=w_sb[r:P:4, k], in_=rows[r])
         nc.sync.dma_start(out=bias_sb[:], in_=bias)
@@ -131,378 +90,331 @@ def tile_temporalaugmentedbilinear_t_kernel(tc, x_bytes, x_scale, w1, g, w, w2, 
         ident_b = keep.tile([P, P], BF16, name="ident_b", align_bytes=64)
         nc.scalar.activation(out=ident_b[:], in_=ident[:], func=ACT.Copy)
 
-        planes = {}
+        wide = {}
 
-        def slot_views(u, i, lo, hi):
-            if u not in planes:
-                planes[u] = pln.tile([P, 4, width(u)], BF16, name="planes", align_bytes=64)
-            codes = raw[u][:, i, lo:hi].bitcast(FP8)
-            return planes[u][:, i, lo:hi], codes
+        def slot_views(pair, i, lo, hi):
+            if pair not in wide:
+                wide[pair] = wide_pool.tile([P, 4, 2 * T], BF16, name="wide", align_bytes=64)
+            return wide[pair][:, i, lo:hi], raw[pair][:, i, lo:hi].bitcast(FP8)
 
-        def widen_s(u, i, lo=0, hi=None):
-            if u > LAST:
-                return
-            if hi is None:
-                hi = width(u) - (release_columns(u) if i == 3 else 0)
-            wide, codes = slot_views(u, i, lo, hi)
-            nc.scalar.activation(out=wide, in_=codes, func=ACT.Copy, scale=xs[:, i : i + 1])
+        def widen_scalar(pair, i, lo, hi):
+            values, codes = slot_views(pair, i, lo, hi)
+            nc.scalar.activation(out=values, in_=codes, func=ACT.Copy, scale=xs[:, i : i + 1])
 
-        values = {}
+        def widen_vector(pair, i, lo, hi):
+            values, codes = slot_views(pair, i, lo, hi)
+            nc.vector.tensor_scalar(out=values, in0=codes, scalar1=xs[:, i : i + 1], scalar2=None, op0=ALU.mult)
 
-        def cast_s(u):
-            if u <= LAST and cast_runs(u):
-                values[u] = pln.tile([P, 4, 16 * cast_runs(u)], BF16, name="values", align_bytes=64)
-                nc.scalar.copy(
-                    out=values[u][:].rearrange("p i t -> p (i t)"),
-                    in_=raw_cast[u][:].rearrange("p i t -> p (i t)").bitcast(FP8),
-                )
+        def widen_slot(pair, i, lo=0):
+            if pair <= LAST:
+                widen_scalar(pair, i, lo, 2 * T - (RELEASE_COLUMNS if i == 3 else 0))
 
-        def widen_v(u, i, lo, hi):
-            wide, codes = slot_views(u, i, lo, hi)
-            nc.vector.tensor_scalar(out=wide, in0=codes, scalar1=xs[:, i : i + 1], scalar2=None, op0=ALU.mult)
-
-        w1_g = keep.tile([P, 512], BF16, name="w1_g", align_bytes=64)
-        w1_c = keep.tile([P, 128], U32, name="w1_c", align_bytes=64)
-        w1_s = keep.tile([P, 128], U8, name="w1_s", align_bytes=64)
-        w_g = keep.tile([P, 2, Q, 4], BF16, name="w_g", align_bytes=64)
-        w_c = keep.tile([P, 256], U32, name="w_c", align_bytes=64)
-        w_s = keep.tile([P, 256], U8, name="w_s", align_bytes=64)
+        w1_laid = keep.tile([P, 4 * PF], BF16, name="w1_laid", align_bytes=64)
+        w1_codes = keep.tile([P, PF], U32, name="w1_codes", align_bytes=64)
+        w1_scales = keep.tile([P, PF], U8, name="w1_scales", align_bytes=64)
+        w_laid = keep.tile([P, 2, Q, 4], BF16, name="w_laid", align_bytes=64)
+        w_codes = keep.tile([P, 2 * Q], U32, name="w_codes", align_bytes=64)
+        w_scales = keep.tile([P, 2 * Q], U8, name="w_scales", align_bytes=64)
 
         w1_words = w1_sb[:].bitcast(F32)
-        w1_t = ps_h.tile([P, 512], F32, name="h_ps")
-        for u in (0, 1):
-            nc.tensor.transpose(w1_t[:, 128 * u : 128 * (u + 1)], w1_words[:, u : 256 : 2], ident[:])
-        g_t = ps_i.tile([P, P], BF16, name="id_ps")
-        nc.tensor.transpose(g_t[:], g_rows[:], ident_b[:])
+        w1_turned = ps_h.tile([P, T], F32, name="h0")
+        for half in (0, 1):
+            nc.tensor.transpose(w1_turned[:, PF * half : PF * (half + 1)], w1_words[:, half : D // 2 : 2], ident[:])
+        g_turned = ps_laid.tile([P, P], BF16, name="laid_ps")
+        nc.tensor.transpose(g_turned[:], g_rows[:], ident_b[:])
 
-        def prep_w1_copy():
+        def lay_w1():
             nc.vector.tensor_copy(
-                out=w1_g[:].bitcast(F32).rearrange("p (r u) -> p r u", u=2),
-                in_=w1_t[:, 0:256].rearrange("p (u r) -> p r u", u=2),
+                out=w1_laid[:].bitcast(F32).rearrange("p (f half) -> p f half", half=2),
+                in_=w1_turned[:, 0 : 2 * PF].rearrange("p (half f) -> p f half", half=2),
             )
 
-        def prep_w1_quant():
-            nc.vector.quantize_mx(out=w1_c[:].bitcast(FP8X4), scales=w1_s[:], in_=w1_g[:])
+        def quantise_w1():
+            nc.vector.quantize_mx(out=w1_codes[:].bitcast(FP8X4), scales=w1_scales[:], in_=w1_laid[:])
 
-        def prep_w_copy():
-            nc.vector.tensor_copy(out=w_g[:, 0], in_=w_sb[:, 0].rearrange("p j q -> p q j"))
+        def lay_w():
+            nc.vector.tensor_copy(out=w_laid[:, 0], in_=w_sb[:, 0].rearrange("p j q -> p q j"))
             nc.vector.tensor_scalar(
-                out=w_g[:, 1], in0=w_sb[:, 1].rearrange("p j q -> p q j"),
+                out=w_laid[:, 1], in0=w_sb[:, 1].rearrange("p j q -> p q j"),
                 scalar1=-1.0, scalar2=None, op0=ALU.mult,
             )
 
-        def prep_w_quant():
+        def quantise_w():
             nc.vector.quantize_mx(
-                out=w_c[:].bitcast(FP8X4), scales=w_s[:], in_=w_g[:].rearrange("p a q j -> p (a q j)")
+                out=w_codes[:].bitcast(FP8X4), scales=w_scales[:], in_=w_laid[:].rearrange("p k q j -> p (k q j)")
             )
 
         lam128 = keep.tile([P, 1], F32, name="lam128")
-        near0 = keep.tile([P, 1], F32, name="near0")
-        c128 = keep.tile([P, 1], F32, name="c128")
-        rc = keep.tile([P, 1], F32, name="rc")
-        kneg = keep.tile([P, 1], F32, name="kneg")
+        near_zero = keep.tile([P, 1], F32, name="near_zero")
+        c = keep.tile([P, 1], F32, name="c")
+        c_inv = keep.tile([P, 1], F32, name="c_inv")
+        shift = keep.tile([P, 1], F32, name="shift")
         bias_c = keep.tile([P, Q], F32, name="bias_c")
-        consts = ps_c.tile([P, Q + 4], F32, name="consts")
-        bias_ps = consts[:, 0:Q]
-        xs_ps = consts[:, Q : Q + 4]
-        TINY = 1e-16
+        bias_ps = ps_bias.tile([P, Q], F32, name="bias_ps")
 
-        lam_steps = [
-            lambda: nc.vector.tensor_scalar(out=lam128[:], in0=lam_sb[:], scalar1=128.0, scalar2=None, op0=ALU.mult),
-            lambda: nc.vector.tensor_scalar(
-                out=near0[:], in0=lam128[:], scalar1=lam128[:], scalar2=TINY * TINY, op0=ALU.mult, op1=ALU.is_lt
-            ),
-            lambda: nc.vector.scalar_tensor_tensor(
-                out=c128[:], in0=near0[:], scalar=2 * TINY, in1=lam128[:], op0=ALU.mult, op1=ALU.add
-            ),
-            lambda: nc.vector.reciprocal(rc[:], c128[:]),
-            lambda: nc.vector.scalar_tensor_tensor(
-                out=kneg[:], in0=lam_sb[:], scalar=1.0, in1=rc[:], op0=ALU.subtract, op1=ALU.mult
-            ),
-            lambda: nc.vector.tensor_scalar(out=bias_c[:], in0=bias_sb[:], scalar1=rc[:], scalar2=None, op0=ALU.mult),
-        ]
+        def scale_lam():
+            nc.vector.tensor_scalar(out=lam128[:], in0=lam_sb[:], scalar1=128.0, scalar2=None, op0=ALU.mult)
 
-        grouped = {}
-        by_batch = (0, LAST)
-
-        def lay(u, a0, a1):
-            if u not in grouped:
-                grouped[u] = grp.tile([P, 2048 * size(u)], BF16, name="grouped", align_bytes=64)
-            f = cast_runs(u)
-            if a0 < f:
-                src = values[u][:].rearrange("p i (s j r) -> p s j r i", j=4, r=4)[:, a0:a1]
-            else:
-                src = planes[u][:].rearrange("p i (s j r) -> p s j r i", j=4, r=4)[:, a0 - f : a1 - f]
-            if u in by_batch:
-                b = a0 // RUNS
-                part = grouped[u][:, 2048 * b : 2048 * (b + 1)]
-                return src, part.rearrange("p (j s r i) -> p s j r i", j=4, r=4, i=4)[:, a0 - RUNS * b : a1 - RUNS * b]
-            return src, grouped[u][:].rearrange("p (j s r i) -> p s j r i", j=4, r=4, i=4)[:, a0:a1]
-
-        def lay_v(u, a0, a1):
-            if a1 <= a0:
-                return
-            cuts = [a0, RUNS, a1] if u in by_batch and a0 < RUNS < a1 else [a0, a1]
-            for lo, hi in zip(cuts, cuts[1:]):
-                src, dst = (ap.rearrange("p s j r i -> p s j i r") for ap in lay(u, lo, hi))
-                nc.vector.tensor_copy(out=dst, in_=src)
-
-        def lay_scaled(u):
-            if cast_runs(u):
-                src, dst = lay(u, 0, cast_runs(u))
-                nc.vector.tensor_tensor(
-                    out=dst.rearrange("p s j r i -> p s j (r i)"), in0=src.rearrange("p s j r i -> p (s j r) i"),
-                    in1=xs_ps.unsqueeze(1).to_broadcast([P, 16 * cast_runs(u), 4]), op=ALU.mult,
-                )
-
-        def lay_s(u):
-            if scalar_runs(u):
-                src, dst = lay(u, cast_runs(u), cast_runs(u) + scalar_runs(u))
-                nc.scalar.copy(out=dst, in_=src)
-
-        def first_tensor_run(u):
-            return RUNS * size(u) - gpsimd_runs(u) - tensor_runs(u)
-
-        def lay_g(u):
-            src, dst = lay(u, RUNS * size(u) - gpsimd_runs(u), RUNS * size(u))
-            nc.gpsimd.tensor_scalar(out=dst, in0=src, scalar1=1.0, scalar2=0.0, op0=ALU.mult, op1=ALU.add)
-
-        id_ps = {}
-
-        def lay_t(u):
-            for h in range(size(u) // 2):
-                id_ps[u, h] = ps_i.tile([P, 2, 64 * TENSOR_RUNS], BF16, name="id_ps")
-                for k in (0, 1):
-                    a0 = first_tensor_run(u) + TENSOR_RUNS * (2 * h + k)
-                    src, dst = lay(u, a0, a0 + TENSOR_RUNS)
-                    nc.tensor.matmul(
-                        id_ps[u, h][:, k].rearrange("p (t i) -> p t i", i=4), lhsT=ident_b[:],
-                        rhs=src.rearrange("p s j r i -> p (s j r) i"), start=True, stop=True,
-                    )
-
-        def lay_out(u, h, copy):
-            if h < size(u) // 2:
-                a0 = first_tensor_run(u) + 2 * TENSOR_RUNS * h
-                src, dst = lay(u, a0, a0 + 2 * TENSOR_RUNS)
-                copy(
-                    out=dst.rearrange("p s j r i -> p s j (r i)"),
-                    in_=id_ps[u, h][:].rearrange("p k (s j c) -> p (k s) j c", j=4, c=16),
-                )
-
-        xc, xsc, h_ps, hg = {}, {}, {}, {}
-
-        def quant(u, lo, hi):
-            if u not in xc:
-                xc[u] = cod.tile([P, 512 * size(u)], U32, name="xc", align_bytes=64)
-                xsc[u] = cod.tile([P, 512 * size(u)], U8, name="xsc", align_bytes=64)
-            nc.vector.quantize_mx(
-                out=xc[u][:, lo // 4 : hi // 4].bitcast(FP8X4), scales=xsc[u][:, lo // 4 : hi // 4],
-                in_=grouped[u][:, lo:hi],
+        def find_near_zero():
+            nc.vector.tensor_scalar(
+                out=near_zero[:], in0=lam128[:], scalar1=lam128[:], scalar2=TINY * TINY, op0=ALU.mult, op1=ALU.is_lt
             )
 
-        def features(u, r):
-            h_ps[u, r] = ps_h.tile([P, 512], F32, name="h_ps")
+        def make_c():
+            nc.vector.scalar_tensor_tensor(
+                out=c[:], in0=near_zero[:], scalar=2 * TINY, in1=lam128[:], op0=ALU.mult, op1=ALU.add
+            )
+
+        def make_shift():
+            nc.vector.scalar_tensor_tensor(
+                out=shift[:], in0=lam_sb[:], scalar=1.0, in1=c_inv[:], op0=ALU.subtract, op1=ALU.mult
+            )
+
+        def scale_bias():
+            nc.vector.tensor_scalar(out=bias_c[:], in0=bias_sb[:], scalar1=c_inv[:], scalar2=None, op0=ALU.mult)
+
+        laid = {}
+        by_batch = (0, LAST)
+
+        def run_views(pair, lo, hi):
+            if pair not in laid:
+                laid[pair] = laid_pool.tile([P, 2 * BATCH_COLUMNS], BF16, name="laid", align_bytes=64)
+            src = wide[pair][:].rearrange("p i (s j r) -> p s j r i", j=4, r=4)[:, lo:hi]
+            region, first = laid[pair][:], 0
+            if pair in by_batch:
+                b = lo // RUNS
+                region, first = region[:, BATCH_COLUMNS * b : BATCH_COLUMNS * (b + 1)], RUNS * b
+            dst = region.rearrange("p (j s r i) -> p s j r i", j=4, r=4, i=4)
+            return src, dst[:, lo - first : hi - first]
+
+        def lay_vector(pair, lo, hi):
+            src, dst = (ap.rearrange("p s j r i -> p s j i r") for ap in run_views(pair, lo, hi))
+            nc.vector.tensor_copy(out=dst, in_=src)
+
+        def lay_scalar(pair, lo, hi):
+            src, dst = run_views(pair, lo, hi)
+            nc.scalar.copy(out=dst, in_=src)
+
+        def first_gpsimd_run(pair):
+            return 2 * RUNS - gpsimd_runs(pair)
+
+        def first_tensor_run(pair):
+            return first_gpsimd_run(pair) - 2 * TENSOR_RUNS
+
+        def release_gpsimd(pair):
+            widen_vector(pair, 3, 2 * T - RELEASE_COLUMNS, 2 * T)
+            src, dst = run_views(pair, first_gpsimd_run(pair), 2 * RUNS)
+            nc.gpsimd.tensor_scalar(out=dst, in0=src, scalar1=1.0, scalar2=0.0, op0=ALU.mult, op1=ALU.add)
+
+        laid_ps = {}
+
+        def lay_tensor(pair):
+            laid_ps[pair] = ps_laid.tile([P, 2, 64 * TENSOR_RUNS], BF16, name="laid_ps")
+            for k in (0, 1):
+                lo = first_tensor_run(pair) + TENSOR_RUNS * k
+                src, dst = run_views(pair, lo, lo + TENSOR_RUNS)
+                nc.tensor.matmul(
+                    laid_ps[pair][:, k].rearrange("p (t i) -> p t i", i=4), lhsT=ident_b[:],
+                    rhs=src.rearrange("p s j r i -> p (s j r) i"), start=True, stop=True,
+                )
+
+        def copy_out_laid(pair):
+            src, dst = run_views(pair, first_tensor_run(pair), first_gpsimd_run(pair))
+            nc.vector.tensor_copy(
+                out=dst.rearrange("p s j r i -> p s j (r i)"),
+                in_=laid_ps[pair][:].rearrange("p k (s j n) -> p (k s) j n", j=4, n=16),
+            )
+
+        x_codes, x_scales, h0, h = {}, {}, {}, {}
+
+        def quantise_x(pair, lo, hi):
+            if pair not in x_codes:
+                x_codes[pair] = code_pool.tile([P, 2 * T], U32, name="x_codes", align_bytes=64)
+                x_scales[pair] = code_pool.tile([P, 2 * T], U8, name="x_scales", align_bytes=64)
+            nc.vector.quantize_mx(
+                out=x_codes[pair][:, lo // 4 : hi // 4].bitcast(FP8X4), scales=x_scales[pair][:, lo // 4 : hi // 4],
+                in_=laid[pair][:, lo:hi],
+            )
+
+        def stage1(pair, b):
+            h0[pair, b] = ps_h.tile([P, T], F32, name="h0")
             for j in range(4):
-                tile = 4 * r + j if u in by_batch else size(u) * j + r
-                cols = slice(128 * tile, 128 * (tile + 1))
+                place = 4 * b + j if pair in by_batch else 2 * j + b
+                cols = slice(P * place, P * (place + 1))
                 nc.tensor.matmul_mx(
-                    out=h_ps[u, r][:, 128 * j : 128 * (j + 1)],
-                    lhsT=xc[u][:, cols].bitcast(FP8X4), lhsT_scale=xsc[u][:, cols],
-                    rhs=w1_c[:].bitcast(FP8X4), rhs_scale=w1_s[:],
+                    out=h0[pair, b][:, PF * j : PF * (j + 1)],
+                    lhsT=x_codes[pair][:, cols].bitcast(FP8X4), lhsT_scale=x_scales[pair][:, cols],
+                    rhs=w1_codes[:].bitcast(FP8X4), rhs_scale=w1_scales[:],
                     start=True, stop=True,
                 )
 
-        def gain(u, r):
-            if r >= size(u):
-                return
-            if r == 0:
-                hg[u] = hp.tile([P, size(u), PF, 4], BF16, name="hg", align_bytes=64)
+        def gain(pair, b):
+            if b == 0:
+                h[pair] = h_pool.tile([P, 2, PF, 4], BF16, name="h", align_bytes=64)
             nc.vector.tensor_tensor(
-                out=hg[u][:, r],
-                in0=h_ps[u, r][:].rearrange("p (j f) -> p f j", j=4),
+                out=h[pair][:, b],
+                in0=h0[pair, b][:].rearrange("p (j f) -> p f j", j=4),
                 in1=g_sb[:].unsqueeze(1).to_broadcast([P, PF, 4]),
                 op=ALU.mult,
             )
 
-        ue, mn, sm, kn, rs, ex = {}, {}, {}, {}, {}, {}
+        ue, neg_max, total, offset, total_inv, work = {}, {}, {}, {}, {}, {}
 
-        def banks(n):
-            return [(k, min(2, n - k)) for k in range(0, n, 2)]
-
-        def hquant(part):
-            u, r0, n = part
-            hc = hp.tile([P, n * PF], U32, name="hc", align_bytes=64)
-            hs = hp.tile([P, n * PF], U8, name="hs", align_bytes=64)
+        def stage2(part):
+            pair, b0, n = part
+            h_codes = h_pool.tile([P, n * PF], U32, name="h_codes", align_bytes=64)
+            h_scales = h_pool.tile([P, n * PF], U8, name="h_scales", align_bytes=64)
             nc.vector.quantize_mx(
-                out=hc[:].bitcast(FP8X4), scales=hs[:], in_=hg[u][:, r0 : r0 + n].rearrange("p b f j -> p (b f j)")
+                out=h_codes[:].bitcast(FP8X4), scales=h_scales[:],
+                in_=h[pair][:, b0 : b0 + n].rearrange("p b f j -> p (b f j)"),
             )
-            for k0, m in banks(n):
-                if u == LAST:
-                    bank = ps_h.tile([P, m, 2, Q], F32, name="h_ps")
-                else:
-                    bank = ps_ue.tile([P, m, 2, Q], F32, name="ue")
-                ue[part, k0] = bank
-                for k in range(m):
-                    cols = slice(PF * (k0 + k), PF * (k0 + k + 1))
-                    nc.tensor.matmul_mx(
-                        out=bank[:, k].rearrange("p a q -> p (a q)"),
-                        lhsT=hc[:, cols].bitcast(FP8X4), lhsT_scale=hs[:, cols],
-                        rhs=w_c[:].bitcast(FP8X4), rhs_scale=w_s[:],
-                        start=True, stop=True,
-                    )
+            ue[part] = ps_ue.tile([P, n, 2, Q], F32, name="ue")
+            for k in range(n):
+                cols = slice(PF * k, PF * (k + 1))
+                nc.tensor.matmul_mx(
+                    out=ue[part][:, k].rearrange("p a q -> p (a q)"),
+                    lhsT=h_codes[:, cols].bitcast(FP8X4), lhsT_scale=h_scales[:, cols],
+                    rhs=w_codes[:].bitcast(FP8X4), rhs_scale=w_scales[:],
+                    start=True, stop=True,
+                )
 
         def row_max(part):
-            mn[part] = ep.tile([P, part[2]], F32, name="mn")
-            for k0, m in banks(part[2]):
-                nc.vector.tensor_reduce(out=mn[part][:, k0 : k0 + m], in_=ue[part, k0][:, :, 1], axis=AX.X, op=ALU.min)
+            neg_max[part] = tail_pool.tile([P, part[2]], F32, name="neg_max")
+            nc.vector.tensor_reduce(out=neg_max[part][:], in_=ue[part][:, :, 1], axis=AX.X, op=ALU.min)
 
         def exps(part):
-            sm[part] = ep.tile([P, part[2]], F32, name="sm")
-            ex[part] = ep.tile([P, part[2], Q], F32, name="ex")
+            total[part] = tail_pool.tile([P, part[2]], F32, name="total")
+            work[part] = tail_pool.tile([P, part[2], Q], F32, name="work")
             for k in range(part[2]):
                 nc.scalar.activation(
-                    out=ex[part][:, k], in_=ue[part, k - k % 2][:, k % 2, 1], func=ACT.Exp,
-                    bias=mn[part][:, k : k + 1], scale=-1.0, accum_out=sm[part][:, k : k + 1],
+                    out=work[part][:, k], in_=ue[part][:, k, 1], func=ACT.Exp,
+                    bias=neg_max[part][:, k : k + 1], scale=-1.0, accum_out=total[part][:, k : k + 1],
                 )
 
         def offsets(part):
-            kn[part] = ep.tile([P, part[2]], F32, name="kn")
-            nc.scalar.activation(out=kn[part][:], in_=sm[part][:], func=ACT.Copy, scale=kneg[:])
+            offset[part] = tail_pool.tile([P, part[2]], F32, name="offset")
+            nc.scalar.activation(out=offset[part][:], in_=total[part][:], func=ACT.Copy, scale=shift[:])
 
         def invert(part):
-            rs[part] = ep.tile([P, part[2]], F32, name="rs")
-            nc.vector.reciprocal(rs[part][:], sm[part][:])
+            total_inv[part] = tail_pool.tile([P, part[2]], F32, name="total_inv")
+            nc.vector.reciprocal(total_inv[part][:], total[part][:])
 
         def weigh(part):
             for k in range(part[2]):
                 nc.vector.scalar_tensor_tensor(
-                    out=ex[part][:, k], in0=ex[part][:, k], scalar=kn[part][:, k : k + 1],
-                    in1=ue[part, k - k % 2][:, k % 2, 0], op0=ALU.subtract, op1=ALU.mult,
+                    out=work[part][:, k], in0=work[part][:, k], scalar=offset[part][:, k : k + 1],
+                    in1=ue[part][:, k, 0], op0=ALU.subtract, op1=ALU.mult,
                 )
 
         def mix(part):
             for k in range(part[2]):
                 nc.vector.scalar_tensor_tensor(
-                    out=ex[part][:, k], in0=ex[part][:, k], scalar=rs[part][:, k : k + 1],
-                    in1=bias_ps, op0=ALU.mult, op1=ALU.add,
+                    out=work[part][:, k], in0=work[part][:, k], scalar=total_inv[part][:, k : k + 1],
+                    in1=bias_ps[:], op0=ALU.mult, op1=ALU.add,
                 )
 
         def finish(part):
-            u, r0, n = part
-            o = ep.tile([P, n, Q], F32, name="o")
-            nc.scalar.activation(out=o[:], in_=ex[part][:], func=ACT.Tanh, scale=c128[:])
-            b0 = first_batch[u] + r0
-            nc.sync.dma_start(out=out[b0 : b0 + n].rearrange("b p q -> p b q"), in_=o[:])
+            pair, b0, n = part
+            result = tail_pool.tile([P, n, Q], F32, name="result")
+            nc.scalar.activation(out=result[:], in_=work[part][:], func=ACT.Tanh, scale=c[:])
+            rows = slice(2 * pair + b0, 2 * pair + b0 + n)
+            nc.sync.dma_start(out=out[rows].rearrange("b p q -> p b q"), in_=result[:])
 
-        def whole(u, stage):
-            if u >= 0:
-                stage((u, 0, size(u)))
+        def whole(pair, stage):
+            if pair >= 0:
+                stage((pair, 0, 2))
 
-        for r in (0, 1):
+        for b, row_step in enumerate((scale_lam, find_near_zero)):
             for i in range(4):
-                widen = widen_v if i < 3 - r else widen_s
-                widen(0, i, r * T, (r + 1) * T)
-            lam_steps[r]()
+                widen = widen_vector if i < 3 - b else widen_scalar
+                widen(0, i, b * T, (b + 1) * T)
+            row_step()
         for i in range(4):
-            widen_s(1, i, 0, width(1) - T)
+            widen_scalar(1, i, 0, T)
         for i in range(1, 4):
-            widen_s(1, i, width(1) - T)
-        lay_v(0, 0, RUNS)
-        lam_steps[2]()
-        prep_w1_copy()
-        lay_v(0, RUNS, 2 * RUNS)
-        lam_steps[3]()
-        prep_w1_quant()
-        for i in range(1):
-            widen_v(1, i, T, 2 * T)
+            widen_slot(1, i, T)
+        lay_vector(0, 0, RUNS)
+        make_c()
+        lay_w1()
+        lay_vector(0, RUNS, 2 * RUNS)
+        nc.vector.reciprocal(c_inv[:], c[:])
+        quantise_w1()
+        widen_vector(1, 0, T, 2 * T)
 
-        def release(u):
-            widen_v(u, 3, width(u) - release_columns(u), width(u))
-            lay_g(u)
+        for n in range(LAST):
+            before_last = n + 1 == LAST
+            load(n + 3)
+            widen_slot(n + 2, 0)
+            if before_last:
+                lay_scalar(LAST, 0, SCALAR_LAST_RUNS)
+            whole(n - 3, finish)
+            whole(n - 2, offsets)
 
-        for u in range(LAST):
-            n = size(u)
-            early = cast_runs(u + 1) > 0
-            load(u + 3)
-            widen_s(u + 2, 0)
-            lay_s(u + 1)
-            if u == 1:
-                prep_w_copy()
-            if 0 < u < LAST - 1:
-                lay_t(u + 1)
-            if u == 1:
-                lam_steps[5]()
-                prep_w_quant()
-            whole(u - 1, hquant)
-            whole(u - 2, invert)
-            if early:
-                release(u + 1)
-            if u == 0:
-                quant(0, 0, 2048)
-                quant(0, 2048, 4096)
+            if n == 1:
+                lay_w()
+            if n > 0 and not before_last:
+                lay_tensor(n + 1)
+            if n == 1:
+                scale_bias()
+                quantise_w()
+            whole(n - 1, stage2)
+            if n == 0:
+                quantise_x(0, 0, BATCH_COLUMNS)
+                quantise_x(0, BATCH_COLUMNS, 2 * BATCH_COLUMNS)
             else:
-                quant(u, 0, 4096)
-            features(u, 0)
-            features(u, 1)
-            if u == 0:
-                lay_t(1)
-                lam_steps[4]()
-                nc.vector.tensor_copy(out=g_sb[:], in_=g_t[:, 0:4])
-            widen_s(u + 2, 1)
-            widen_s(u + 2, 2)
-            if not early:
-                release(u + 1)
-            lay_v(u + 1, cast_runs(u + 1) + scalar_runs(u + 1), first_tensor_run(u + 1) if u + 1 < LAST else RUNS)
-            lay_scaled(u + 1)
-            if u == 1:
-                nc.tensor.matmul(bias_ps, lhsT=ident[:], rhs=bias_c[:], start=True, stop=True)
-            whole(u - 1, row_max)
-            whole(u - 1, exps)
-            if u + 1 == LAST:
-                src, dst = lay(LAST, RUNS, first_tensor_run(LAST))
-                nc.scalar.copy(out=dst, in_=src)
-            whole(u - 2, mix)
-            if not scalar_empties(u + 1) and u > 0:
-                lay_out(u + 1, 0, nc.vector.tensor_copy)
-            gain(u, 0)
-            if u == 0:
-                lay_out(u + 1, 0, nc.vector.tensor_copy)
-            if n == 4:
-                features(u, 3)
-            whole(u - 2, finish)
-            whole(u - 1, offsets)
-            gain(u, 1)
-            gain(u, 2)
-            if not scalar_empties(u + 1):
-                lay_out(u + 1, 1, nc.vector.tensor_copy)
-            gain(u, 3)
-            if u < LAST - 1:
-                whole(u - 1, weigh)
-            widen_s(u + 2, 3)
+                quantise_x(n, 0, 2 * BATCH_COLUMNS)
+            stage1(n, 0)
+            stage1(n, 1)
+            if n == 0:
+                lay_tensor(1)
+                make_shift()
+                nc.vector.tensor_copy(out=g_sb[:], in_=g_turned[:, 0:4])
+            for i in range(1, 4):
+                widen_slot(n + 2, i)
+            whole(n - 2, invert)
+            release_gpsimd(n + 1)
+            if before_last:
+                lay_vector(LAST, SCALAR_LAST_RUNS, RUNS)
+            else:
+                lay_vector(n + 1, 0, first_tensor_run(n + 1))
+            if n == 1:
+                nc.tensor.matmul(bias_ps[:], lhsT=ident[:], rhs=bias_c[:], start=True, stop=True)
+
+            whole(n - 1, row_max)
+            whole(n - 1, exps)
+            if before_last:
+                lay_scalar(LAST, RUNS, first_gpsimd_run(LAST))
+            whole(n - 2, weigh)
+            gain(n, 0)
+            gain(n, 1)
+            if not before_last:
+                copy_out_laid(n + 1)
+            whole(n - 2, mix)
 
         first, second = (LAST, 0, 1), (LAST, 1, 1)
-        whole(LAST - 1, hquant)
-        quant(LAST, 0, 2048)
-        features(LAST, 0)
+        whole(LAST - 2, offsets)
+        whole(LAST - 1, stage2)
+        quantise_x(LAST, 0, BATCH_COLUMNS)
+        stage1(LAST, 0)
         whole(LAST - 2, invert)
-        quant(LAST, 2048, 4096)
-        features(LAST, 1)
+        whole(LAST - 3, finish)
+        quantise_x(LAST, BATCH_COLUMNS, 2 * BATCH_COLUMNS)
+        stage1(LAST, 1)
         whole(LAST - 1, row_max)
         whole(LAST - 1, exps)
         whole(LAST - 2, weigh)
         gain(LAST, 0)
         whole(LAST - 1, offsets)
         gain(LAST, 1)
-        hquant(first)
+        stage2(first)
         whole(LAST - 2, mix)
         whole(LAST - 2, finish)
-        hquant(second)
+        stage2(second)
         whole(LAST - 1, invert)
         whole(LAST - 1, weigh)
-        row_max(first)
-        exps(first)
-        row_max(second)
-        exps(second)
+        for part in (first, second):
+            row_max(part)
+            exps(part)
         offsets(first)
         whole(LAST - 1, mix)
         offsets(second)
@@ -511,7 +423,6 @@ def tile_temporalaugmentedbilinear_t_kernel(tc, x_bytes, x_scale, w1, g, w, w2, 
         invert(second)
         whole(LAST - 1, finish)
         weigh(second)
-        mix(first)
-        mix(second)
-        finish(first)
-        finish(second)
+        for stage in (mix, finish):
+            stage(first)
+            stage(second)

@@ -21,13 +21,13 @@ LAST = B // 2 - 1
 RUNS = T // 16
 BATCH_COLUMNS = 4 * T
 TENSOR_RUNS = 5
-RELEASE_COLUMNS = 96
+RELEASE_COLUMNS = 192
 SCALAR_LAST_RUNS = 22
 TINY = 1e-16
 
 
 def gpsimd_runs(pair):
-    return {1: 14, 2: 18, LAST: 18}.get(pair, 24)
+    return {1: 16, 2: 20, LAST: 20}.get(pair, 28)
 
 
 def tile_temporalaugmentedbilinear_t_kernel(tc, x_bytes, x_scale, w1, g, w, w2, lam, bias, out):
@@ -386,9 +386,11 @@ def tile_temporalaugmentedbilinear_t_kernel(tc, x_bytes, x_scale, w1, g, w, w2, 
                 lay_scalar(LAST, RUNS, first_gpsimd_run(LAST))
             whole(n - 2, weigh)
             gain(n, 0)
-            gain(n, 1)
-            if not before_last:
+            if n > 0 and not before_last:
                 copy_out_laid(n + 1)
+            gain(n, 1)
+            if n == 0:
+                copy_out_laid(1)
             whole(n - 2, mix)
 
         first, second = (LAST, 0, 1), (LAST, 1, 1)

@@ -21,13 +21,17 @@ LAST = B // 2 - 1
 RUNS = T // 16
 BATCH_COLUMNS = 4 * T
 TENSOR_RUNS = 5
-RELEASE_COLUMNS = 192
+RELEASE_COLUMNS = 224
 SCALAR_LAST_RUNS = 22
 TINY = 1e-16
 
 
+def tensor_runs(pair):
+    return 2 * TENSOR_RUNS + (1 if 3 <= pair < LAST - 1 else 0)
+
+
 def gpsimd_runs(pair):
-    return {1: 16, 2: 20, LAST: 20}.get(pair, 28)
+    return {1: 18, 2: 22, LAST - 1: 28, LAST: 20}.get(pair, 29)
 
 
 def tile_temporalaugmentedbilinear_t_kernel(tc, x_bytes, x_scale, w1, g, w, w2, lam, bias, out):
@@ -199,7 +203,7 @@ def tile_temporalaugmentedbilinear_t_kernel(tc, x_bytes, x_scale, w1, g, w, w2, 
             return 2 * RUNS - gpsimd_runs(pair)
 
         def first_tensor_run(pair):
-            return first_gpsimd_run(pair) - 2 * TENSOR_RUNS
+            return first_gpsimd_run(pair) - tensor_runs(pair)
 
         def release_gpsimd(pair):
             widen_vector(pair, 3, 2 * T - RELEASE_COLUMNS, 2 * T)
@@ -209,12 +213,11 @@ def tile_temporalaugmentedbilinear_t_kernel(tc, x_bytes, x_scale, w1, g, w, w2, 
         laid_ps = {}
 
         def lay_tensor(pair):
-            laid_ps[pair] = ps_laid.tile([P, 2, 64 * TENSOR_RUNS], BF16, name="laid_ps")
-            for k in (0, 1):
-                lo = first_tensor_run(pair) + TENSOR_RUNS * k
-                src, dst = run_views(pair, lo, lo + TENSOR_RUNS)
+            laid_ps[pair] = ps_laid.tile([P, 64 * tensor_runs(pair)], BF16, name="laid_ps")
+            for lo, hi in ((0, TENSOR_RUNS), (TENSOR_RUNS, tensor_runs(pair))):
+                src, dst = run_views(pair, first_tensor_run(pair) + lo, first_tensor_run(pair) + hi)
                 nc.tensor.matmul(
-                    laid_ps[pair][:, k].rearrange("p (t i) -> p t i", i=4), lhsT=ident_b[:],
+                    laid_ps[pair][:, 64 * lo : 64 * hi].rearrange("p (t i) -> p t i", i=4), lhsT=ident_b[:],
                     rhs=src.rearrange("p s j r i -> p (s j r) i"), start=True, stop=True,
                 )
 
@@ -222,7 +225,7 @@ def tile_temporalaugmentedbilinear_t_kernel(tc, x_bytes, x_scale, w1, g, w, w2, 
             src, dst = run_views(pair, first_tensor_run(pair), first_gpsimd_run(pair))
             nc.vector.tensor_copy(
                 out=dst.rearrange("p s j r i -> p s j (r i)"),
-                in_=laid_ps[pair][:].rearrange("p k (s j n) -> p (k s) j n", j=4, n=16),
+                in_=laid_ps[pair][:].rearrange("p (s j n) -> p s j n", j=4, n=16),
             )
 
         x_codes, x_scales, h0, h = {}, {}, {}, {}
@@ -386,11 +389,11 @@ def tile_temporalaugmentedbilinear_t_kernel(tc, x_bytes, x_scale, w1, g, w, w2, 
                 lay_scalar(LAST, RUNS, first_gpsimd_run(LAST))
             whole(n - 2, weigh)
             gain(n, 0)
-            if n > 0 and not before_last:
+            if n > 1 and not before_last:
                 copy_out_laid(n + 1)
             gain(n, 1)
-            if n == 0:
-                copy_out_laid(1)
+            if n <= 1:
+                copy_out_laid(n + 1)
             whole(n - 2, mix)
 
         first, second = (LAST, 0, 1), (LAST, 1, 1)

@@ -20,18 +20,18 @@ P = 128
 LAST = B // 2 - 1
 RUNS = T // 16
 BATCH_COLUMNS = 4 * T
-TENSOR_RUNS = 5
+TENSOR_RUNS = 6
 RELEASE_COLUMNS = 224
 SCALAR_LAST_RUNS = 22
 TINY = 1e-16
 
 
 def tensor_runs(pair):
-    return 2 * TENSOR_RUNS + (1 if 3 <= pair < LAST - 1 else 0)
+    return 12 if pair % 2 == 0 and 3 <= pair < LAST - 1 else 10
 
 
 def gpsimd_runs(pair):
-    return {1: 18, 2: 22, LAST - 1: 28, LAST: 20}.get(pair, 29)
+    return {1: 18, 2: 22, LAST - 1: 28, LAST: 20}.get(pair, 28)
 
 
 def tile_temporalaugmentedbilinear_t_kernel(tc, x_bytes, x_scale, w1, g, w, w2, lam, bias, out):
@@ -81,12 +81,12 @@ def tile_temporalaugmentedbilinear_t_kernel(tc, x_bytes, x_scale, w1, g, w, w2, 
         load(2)
         nc.gpsimd.memset(g_rows[:], 0.0)
         nc.sync.dma_start(
-            out=g_rows[0:4, :].rearrange("j (s r) -> j s r", r=4), in_=g.rearrange("(s j r) -> j s r", j=4, r=4)
+            out=g_rows[0:4, :].rearrange("j (a r) -> j a r", r=8), in_=g.rearrange("(a j r) -> j a r", j=4, r=8)
         )
         for k, weight in enumerate((w2, w)):
-            rows = weight.rearrange("(s j r) q -> r s j q", j=4, r=4)
-            for r in range(4):
-                nc.sync.dma_start(out=w_sb[r:P:4, k], in_=rows[r])
+            rows = weight.rearrange("(a j r) q -> r a j q", j=4, r=8)
+            for r in range(8):
+                nc.sync.dma_start(out=w_sb[r:P:8, k], in_=rows[r])
         nc.sync.dma_start(out=bias_sb[:], in_=bias)
 
         ident = keep.tile([P, P], F32, name="ident")
@@ -183,16 +183,16 @@ def tile_temporalaugmentedbilinear_t_kernel(tc, x_bytes, x_scale, w1, g, w, w2, 
         def run_views(pair, lo, hi):
             if pair not in laid:
                 laid[pair] = laid_pool.tile([P, 2 * BATCH_COLUMNS], BF16, name="laid", align_bytes=64)
-            src = wide[pair][:].rearrange("p i (s j r) -> p s j r i", j=4, r=4)[:, lo:hi]
+            src = wide[pair][:].rearrange("p i (s j r) -> p s j r i", j=4, r=8)[:, lo // 2 : hi // 2]
             region, first = laid[pair][:], 0
             if pair in by_batch:
                 b = lo // RUNS
                 region, first = region[:, BATCH_COLUMNS * b : BATCH_COLUMNS * (b + 1)], RUNS * b
-            dst = region.rearrange("p (j s r i) -> p s j r i", j=4, r=4, i=4)
-            return src, dst[:, lo - first : hi - first]
+            dst = region.rearrange("p (j s r i) -> p s j r i", j=4, r=8, i=4)
+            return src, dst[:, (lo - first) // 2 : (hi - first) // 2]
 
         def lay_vector(pair, lo, hi):
-            src, dst = (ap.rearrange("p s j r i -> p s j i r") for ap in run_views(pair, lo, hi))
+            src, dst = (ap.rearrange("p s j r i -> p j s i r") for ap in run_views(pair, lo, hi))
             nc.vector.tensor_copy(out=dst, in_=src)
 
         def lay_scalar(pair, lo, hi):
@@ -225,7 +225,7 @@ def tile_temporalaugmentedbilinear_t_kernel(tc, x_bytes, x_scale, w1, g, w, w2, 
             src, dst = run_views(pair, first_tensor_run(pair), first_gpsimd_run(pair))
             nc.vector.tensor_copy(
                 out=dst.rearrange("p s j r i -> p s j (r i)"),
-                in_=laid_ps[pair][:].rearrange("p (s j n) -> p s j n", j=4, n=16),
+                in_=laid_ps[pair][:].rearrange("p (s j n) -> p s j n", j=4, n=32),
             )
 
         x_codes, x_scales, h0, h = {}, {}, {}, {}

@@ -21,8 +21,9 @@ LAST = B // 2 - 1
 RUNS = T // 16
 BATCH_COLUMNS = 4 * T
 TENSOR_RUNS = 6
-RELEASE_COLUMNS = 224
+RELEASE_COLUMNS = 288
 SCALAR_LAST_RUNS = 22
+EARLY_RUNS = 16
 TINY = 1e-16
 
 
@@ -31,7 +32,7 @@ def tensor_runs(pair):
 
 
 def gpsimd_runs(pair):
-    return {1: 18, 2: 22, LAST - 1: 28, LAST: 20}.get(pair, 28)
+    return {1: 18, 2: 22, LAST - 1: 28, LAST: 24}.get(pair, 28)
 
 
 def tile_temporalaugmentedbilinear_t_kernel(tc, x_bytes, x_scale, w1, g, w, w2, lam, bias, out):
@@ -60,8 +61,10 @@ def tile_temporalaugmentedbilinear_t_kernel(tc, x_bytes, x_scale, w1, g, w, w2, 
 
         def load(pair):
             if pair <= LAST:
-                load_batch(pair, 0)
-                load_batch(pair, 1)
+                raw[pair] = raw_pool.tile([P, 4, 2 * T], U8, name="raw", align_bytes=64)
+                rows = x_bytes[2 * pair : 2 * pair + 2].rearrange("b (p i) t -> p i b t", i=4)
+                for i in range(4):
+                    nc.sync.dma_start(out=raw[pair][:, i].rearrange("p (b t) -> p b t", b=2), in_=rows[:, i])
 
         xs = keep.tile([P, 4], F32, name="xs")
         w1_sb = keep.tile([P, D], BF16, name="w1_sb", align_bytes=64)
@@ -77,7 +80,8 @@ def tile_temporalaugmentedbilinear_t_kernel(tc, x_bytes, x_scale, w1, g, w, w2, 
         load_batch(0, 0, slice(2, 4))
         load_batch(0, 1)
         nc.sync.dma_start(out=w1_sb[:], in_=w1)
-        load(1)
+        load_batch(1, 0)
+        load_batch(1, 1)
         load(2)
         nc.gpsimd.memset(g_rows[:], 0.0)
         nc.sync.dma_start(
@@ -239,9 +243,10 @@ def tile_temporalaugmentedbilinear_t_kernel(tc, x_bytes, x_scale, w1, g, w, w2, 
                 in_=laid[pair][:, lo:hi],
             )
 
-        def stage1(pair, b):
-            h0[pair, b] = ps_h.tile([P, T], F32, name="h0")
-            for j in range(4):
+        def stage1(pair, b, tiles=range(4)):
+            if (pair, b) not in h0:
+                h0[pair, b] = ps_h.tile([P, T], F32, name="h0")
+            for j in tiles:
                 place = 4 * b + j if pair in by_batch else 2 * j + b
                 cols = slice(P * place, P * (place + 1))
                 nc.tensor.matmul_mx(
@@ -281,16 +286,52 @@ def tile_temporalaugmentedbilinear_t_kernel(tc, x_bytes, x_scale, w1, g, w, w2, 
                     start=True, stop=True,
                 )
 
+        scores, plain, rest = {}, {}, {}
+
+        def stage2_alone(part):
+            pair, b0, n = part
+            h_codes = h_pool.tile([P, PF], U32, name="h_codes", align_bytes=64)
+            h_scales = h_pool.tile([P, PF], U8, name="h_scales", align_bytes=64)
+            nc.vector.quantize_mx(
+                out=h_codes[:].bitcast(FP8X4), scales=h_scales[:], in_=h[pair][:, b0].rearrange("p f j -> p (f j)")
+            )
+            scores[part] = ps_laid.tile([P, 1, Q], F32, name="laid_ps")
+            plain[part] = ps_h.tile([P, Q], F32, name="h0")
+            for target, k in ((scores[part][:, 0], 1), (plain[part][:], 0)):
+                cols = slice(Q * k, Q * (k + 1))
+                nc.tensor.matmul_mx(
+                    out=target, lhsT=h_codes[:].bitcast(FP8X4), lhsT_scale=h_scales[:],
+                    rhs=w_codes[:, cols].bitcast(FP8X4), rhs_scale=w_scales[:, cols], start=True, stop=True,
+                )
+
+        def e_of(part):
+            return scores[part][:] if part in scores else ue[part][:, :, 1]
+
+        def plain_path(part):
+            rest[part] = tail_pool.tile([P, Q], F32, name="rest")
+            nc.vector.scalar_tensor_tensor(
+                out=rest[part][:], in0=plain[part][:], scalar=shift[:], in1=bias_c[:], op0=ALU.mult, op1=ALU.subtract
+            )
+
+        def weigh_alone(part):
+            nc.vector.tensor_tensor(out=work[part][:, 0], in0=work[part][:, 0], in1=plain[part][:], op=ALU.mult)
+
+        def mix_alone(part):
+            nc.vector.scalar_tensor_tensor(
+                out=work[part][:, 0], in0=work[part][:, 0], scalar=total_inv[part][:], in1=rest[part][:],
+                op0=ALU.mult, op1=ALU.subtract,
+            )
+
         def row_max(part):
             neg_max[part] = tail_pool.tile([P, part[2]], F32, name="neg_max")
-            nc.vector.tensor_reduce(out=neg_max[part][:], in_=ue[part][:, :, 1], axis=AX.X, op=ALU.min)
+            nc.vector.tensor_reduce(out=neg_max[part][:], in_=e_of(part), axis=AX.X, op=ALU.min)
 
         def exps(part):
             total[part] = tail_pool.tile([P, part[2]], F32, name="total")
             work[part] = tail_pool.tile([P, part[2], Q], F32, name="work")
             for k in range(part[2]):
                 nc.scalar.activation(
-                    out=work[part][:, k], in_=ue[part][:, k, 1], func=ACT.Exp,
+                    out=work[part][:, k], in_=e_of(part)[:, k], func=ACT.Exp,
                     bias=neg_max[part][:, k : k + 1], scale=-1.0, accum_out=total[part][:, k : k + 1],
                 )
 
@@ -318,7 +359,7 @@ def tile_temporalaugmentedbilinear_t_kernel(tc, x_bytes, x_scale, w1, g, w, w2, 
 
         def finish(part):
             pair, b0, n = part
-            result = tail_pool.tile([P, n, Q], F32, name="result")
+            result = tail_pool.tile([P, n, Q], F32, name="result", bufs=LAST + 2)
             nc.scalar.activation(out=result[:], in_=work[part][:], func=ACT.Tanh, scale=c[:])
             rows = slice(2 * pair + b0, 2 * pair + b0 + n)
             nc.sync.dma_start(out=out[rows].rearrange("b p q -> p b q"), in_=result[:])
@@ -344,18 +385,15 @@ def tile_temporalaugmentedbilinear_t_kernel(tc, x_bytes, x_scale, w1, g, w, w2, 
         quantise_w1()
         widen_vector(1, 0, T, 2 * T)
 
-        for n in range(LAST):
-            before_last = n + 1 == LAST
+        for n in range(LAST - 1):
             load(n + 3)
             widen_slot(n + 2, 0)
-            if before_last:
-                lay_scalar(LAST, 0, SCALAR_LAST_RUNS)
             whole(n - 3, finish)
             whole(n - 2, offsets)
 
             if n == 1:
                 lay_w()
-            if n > 0 and not before_last:
+            if n > 0:
                 lay_tensor(n + 1)
             if n == 1:
                 scale_bias()
@@ -375,59 +413,77 @@ def tile_temporalaugmentedbilinear_t_kernel(tc, x_bytes, x_scale, w1, g, w, w2, 
             for i in range(1, 4):
                 widen_slot(n + 2, i)
             whole(n - 2, invert)
+            early = EARLY_RUNS if n <= 1 else 0
+            if early:
+                lay_vector(n + 1, 0, early)
             release_gpsimd(n + 1)
-            if before_last:
-                lay_vector(LAST, SCALAR_LAST_RUNS, RUNS)
-            else:
-                lay_vector(n + 1, 0, first_tensor_run(n + 1))
+            lay_vector(n + 1, early, first_tensor_run(n + 1))
             if n == 1:
                 nc.tensor.matmul(bias_ps[:], lhsT=ident[:], rhs=bias_c[:], start=True, stop=True)
 
             whole(n - 1, row_max)
             whole(n - 1, exps)
-            if before_last:
-                lay_scalar(LAST, RUNS, first_gpsimd_run(LAST))
             whole(n - 2, weigh)
             gain(n, 0)
-            if n > 1 and not before_last:
+            if n > 1:
                 copy_out_laid(n + 1)
             gain(n, 1)
             if n <= 1:
                 copy_out_laid(n + 1)
             whole(n - 2, mix)
 
+        n = LAST - 1
+        whole(n - 2, offsets)
+        lay_scalar(LAST, 0, RUNS)
+        whole(n - 3, finish)
+        whole(n - 1, stage2)
+        whole(n - 2, invert)
+        for half in range(2):
+            if half == 1:
+                release_gpsimd(LAST)
+            quantise_x(n, half * BATCH_COLUMNS, (half + 1) * BATCH_COLUMNS)
+            for b in range(2):
+                stage1(n, b, range(2 * half, 2 * half + 2))
+        whole(n - 1, row_max)
+        whole(n - 1, exps)
+        lay_scalar(LAST, RUNS, first_gpsimd_run(LAST))
+        whole(n - 2, weigh)
+        whole(n - 2, mix)
+        whole(n - 1, offsets)
+        whole(n - 2, finish)
+        gain(n, 0)
+        gain(n, 1)
+
         first, second = (LAST, 0, 1), (LAST, 1, 1)
-        whole(LAST - 2, offsets)
-        whole(LAST - 1, stage2)
         quantise_x(LAST, 0, BATCH_COLUMNS)
         stage1(LAST, 0)
-        whole(LAST - 2, invert)
-        whole(LAST - 3, finish)
+        whole(LAST - 1, stage2)
         quantise_x(LAST, BATCH_COLUMNS, 2 * BATCH_COLUMNS)
         stage1(LAST, 1)
-        whole(LAST - 1, row_max)
-        whole(LAST - 1, exps)
+        whole(LAST - 2, invert)
         whole(LAST - 2, weigh)
         gain(LAST, 0)
-        whole(LAST - 1, offsets)
+        whole(LAST - 1, row_max)
+        whole(LAST - 1, exps)
         gain(LAST, 1)
-        stage2(first)
+        stage2_alone(first)
+        whole(LAST - 1, offsets)
+        stage2_alone(second)
         whole(LAST - 2, mix)
         whole(LAST - 2, finish)
-        stage2(second)
         whole(LAST - 1, invert)
         whole(LAST - 1, weigh)
         for part in (first, second):
             row_max(part)
             exps(part)
-        offsets(first)
         whole(LAST - 1, mix)
-        offsets(second)
-        invert(first)
-        weigh(first)
-        invert(second)
+        plain_path(first)
+        plain_path(second)
         whole(LAST - 1, finish)
-        weigh(second)
-        for stage in (mix, finish):
-            stage(first)
-            stage(second)
+        invert(first)
+        weigh_alone(first)
+        invert(second)
+        weigh_alone(second)
+        for part in (first, second):
+            mix_alone(part)
+            finish(part)

@@ -21,7 +21,7 @@ LAST = B // 2 - 1
 RUNS = T // 16
 BATCH_COLUMNS = 4 * T
 TENSOR_RUNS = 6
-RELEASE_COLUMNS = 288
+RELEASE_COLUMNS = 160
 SCALAR_LAST_RUNS = 22
 EARLY_RUNS = 16
 TINY = 1e-16
@@ -76,8 +76,8 @@ def tile_temporalaugmentedbilinear_t_kernel(tc, x_bytes, x_scale, w1, g, w, w2, 
 
         nc.scalar.dma_start(out=xs[:], in_=x_scale.rearrange("o (p i) z -> p (o i z)", i=4))
         nc.scalar.dma_start(out=lam_sb[:], in_=lam.rearrange("(p o) -> p o", o=1))
-        load_batch(0, 0, slice(0, 2))
-        load_batch(0, 0, slice(2, 4))
+        load_batch(0, 0, slice(0, 1))
+        load_batch(0, 0, slice(1, 4))
         load_batch(0, 1)
         nc.sync.dma_start(out=w1_sb[:], in_=w1)
         load_batch(1, 0)
@@ -88,9 +88,9 @@ def tile_temporalaugmentedbilinear_t_kernel(tc, x_bytes, x_scale, w1, g, w, w2, 
             out=g_rows[0:4, :].rearrange("j (a r) -> j a r", r=8), in_=g.rearrange("(a j r) -> j a r", j=4, r=8)
         )
         for k, weight in enumerate((w2, w)):
-            rows = weight.rearrange("(a j r) q -> r a j q", j=4, r=8)
-            for r in range(8):
-                nc.sync.dma_start(out=w_sb[r:P:8, k], in_=rows[r])
+            rows = weight.rearrange("(a j r) q -> j a r q", j=4, r=8)
+            for j in range(4):
+                nc.sync.dma_start(out=w_sb[:, k, j], in_=rows[j])
         nc.sync.dma_start(out=bias_sb[:], in_=bias)
 
         ident = keep.tile([P, P], F32, name="ident")
@@ -362,7 +362,8 @@ def tile_temporalaugmentedbilinear_t_kernel(tc, x_bytes, x_scale, w1, g, w, w2, 
             result = tail_pool.tile([P, n, Q], F32, name="result", bufs=LAST + 2)
             nc.scalar.activation(out=result[:], in_=work[part][:], func=ACT.Tanh, scale=c[:])
             rows = slice(2 * pair + b0, 2 * pair + b0 + n)
-            nc.sync.dma_start(out=out[rows].rearrange("b p q -> p b q"), in_=result[:])
+            queue = nc.scalar if part == (LAST, 1, 1) else nc.sync
+            queue.dma_start(out=out[rows].rearrange("b p q -> p b q"), in_=result[:])
 
         def whole(pair, stage):
             if pair >= 0:
@@ -413,11 +414,11 @@ def tile_temporalaugmentedbilinear_t_kernel(tc, x_bytes, x_scale, w1, g, w, w2, 
             for i in range(1, 4):
                 widen_slot(n + 2, i)
             whole(n - 2, invert)
-            early = EARLY_RUNS if n <= 1 else 0
-            if early:
-                lay_vector(n + 1, 0, early)
+            late = first_tensor_run(n + 1) - (EARLY_RUNS if n <= 1 else 0)
+            if n <= 1:
+                lay_vector(n + 1, late, first_tensor_run(n + 1))
             release_gpsimd(n + 1)
-            lay_vector(n + 1, early, first_tensor_run(n + 1))
+            lay_vector(n + 1, 0, late)
             if n == 1:
                 nc.tensor.matmul(bias_ps[:], lhsT=ident[:], rhs=bias_c[:], start=True, stop=True)
 

@@ -21,7 +21,7 @@ LAST = B // 2 - 1
 RUNS = T // 16
 BATCH_COLUMNS = 4 * T
 TENSOR_RUNS = 6
-RELEASE_COLUMNS = 160
+RELEASE_COLUMNS = 192
 SCALAR_LAST_RUNS = 22
 EARLY_RUNS = 16
 TINY = 1e-16
@@ -32,7 +32,7 @@ def tensor_runs(pair):
 
 
 def gpsimd_runs(pair):
-    return {1: 18, 2: 22, LAST - 1: 28, LAST: 24}.get(pair, 28)
+    return {1: 18, 2: 22, LAST - 1: 28, LAST: 24}.get(pair, 18 + tensor_runs(pair))
 
 
 def tile_temporalaugmentedbilinear_t_kernel(tc, x_bytes, x_scale, w1, g, w, w2, lam, bias, out):
@@ -77,7 +77,8 @@ def tile_temporalaugmentedbilinear_t_kernel(tc, x_bytes, x_scale, w1, g, w, w2, 
         nc.scalar.dma_start(out=xs[:], in_=x_scale.rearrange("o (p i) z -> p (o i z)", i=4))
         nc.scalar.dma_start(out=lam_sb[:], in_=lam.rearrange("(p o) -> p o", o=1))
         load_batch(0, 0, slice(0, 1))
-        load_batch(0, 0, slice(1, 4))
+        load_batch(0, 0, slice(3, 4))
+        load_batch(0, 0, slice(1, 3))
         load_batch(0, 1)
         nc.sync.dma_start(out=w1_sb[:], in_=w1)
         load_batch(1, 0)
@@ -200,7 +201,7 @@ def tile_temporalaugmentedbilinear_t_kernel(tc, x_bytes, x_scale, w1, g, w, w2, 
             nc.vector.tensor_copy(out=dst, in_=src)
 
         def lay_scalar(pair, lo, hi):
-            src, dst = run_views(pair, lo, hi)
+            src, dst = (ap.rearrange("p s j r i -> p s j i r") for ap in run_views(pair, lo, hi))
             nc.scalar.copy(out=dst, in_=src)
 
         def first_gpsimd_run(pair):

from contextlib import ExitStack

import concourse.mybir as mybir
from concourse.masks import make_identity

B, D, T, PF, Q = 32, 512, 512, 128, 128
FLOPS = 2 * B * PF * D * T + 2 * 2 * B * PF * T * Q

F32 = mybir.dt.float32
BF16 = mybir.dt.bfloat16
U32 = mybir.dt.uint32
U8 = mybir.dt.uint8
FP8 = mybir.dt.float8_e4m3fn
FP8X4 = mybir.dt.float8_e4m3fn_x4
ALU = mybir.AluOpType
ACT = mybir.ActivationFunctionType
AX = mybir.AxisListType

P = 128
LAST = B // 2 - 1
RUNS = T // 16
BATCH_COLUMNS = 4 * T
TENSOR_RUNS = 6
RELEASE_COLUMNS = 192
SCALAR_LAST_RUNS = 22
EARLY_RUNS = 16
TINY = 1e-16


def tensor_runs(pair):
    return 12 if pair % 2 == 0 and 3 <= pair < LAST - 1 else 10


def gpsimd_runs(pair):
    return {1: 18, 2: 22, LAST - 1: 28, LAST: 24}.get(pair, 18 + tensor_runs(pair))


def tile_temporalaugmentedbilinear_t_kernel(tc, x_bytes, x_scale, w1, g, w, w2, lam, bias, out):
    nc = tc.nc
    with ExitStack() as ctx:
        keep = ctx.enter_context(tc.tile_pool(name="keep", bufs=1))
        raw_pool = ctx.enter_context(tc.tile_pool(name="raw_pool", bufs=4))
        wide_pool = ctx.enter_context(tc.tile_pool(name="wide_pool", bufs=3))
        laid_pool = ctx.enter_context(tc.tile_pool(name="laid_pool", bufs=2))
        code_pool = ctx.enter_context(tc.tile_pool(name="code_pool", bufs=2))
        h_pool = ctx.enter_context(tc.tile_pool(name="h_pool", bufs=2))
        tail_pool = ctx.enter_context(tc.tile_pool(name="tail_pool", bufs=4))
        ps_h = ctx.enter_context(tc.psum_pool(name="ps_h", bufs=2))
        ps_ue = ctx.enter_context(tc.psum_pool(name="ps_ue", bufs=3))
        ps_laid = ctx.enter_context(tc.psum_pool(name="ps_laid", bufs=2))
        ps_bias = ctx.enter_context(tc.psum_pool(name="ps_bias", bufs=1))
        ctx.enter_context(tc.manual_schedule())

        raw = {}

        def load_batch(pair, b, slots=slice(0, 4)):
            if pair not in raw:
                raw[pair] = raw_pool.tile([P, 4, 2 * T], U8, name="raw", align_bytes=64)
            rows = x_bytes[2 * pair + b].rearrange("(p i) t -> p i t", i=4)
            nc.sync.dma_start(out=raw[pair][:, slots, b * T : (b + 1) * T], in_=rows[:, slots])

        def load(pair):
            if pair <= LAST:
                raw[pair] = raw_pool.tile([P, 4, 2 * T], U8, name="raw", align_bytes=64)
                rows = x_bytes[2 * pair : 2 * pair + 2].rearrange("b (p i) t -> p i b t", i=4)
                for i in range(4):
                    nc.sync.dma_start(out=raw[pair][:, i].rearrange("p (b t) -> p b t", b=2), in_=rows[:, i])

        xs = keep.tile([P, 4], F32, name="xs")
        w1_sb = keep.tile([P, D], BF16, name="w1_sb", align_bytes=64)
        w_sb = keep.tile([P, 2, 4, Q], BF16, name="w_sb", align_bytes=64)
        g_sb = keep.tile([P, 4], BF16, name="g_sb")
        lam_sb = keep.tile([P, 1], BF16, name="lam_sb")
        bias_sb = keep.tile([P, Q], BF16, name="bias_sb")
        g_rows = keep.tile([P, P], BF16, name="g_rows", align_bytes=64)

        nc.scalar.dma_start(out=xs[:], in_=x_scale.rearrange("o (p i) z -> p (o i z)", i=4))
        nc.scalar.dma_start(out=lam_sb[:], in_=lam.rearrange("(p o) -> p o", o=1))
        load_batch(0, 0, slice(0, 1))
        load_batch(0, 0, slice(3, 4))
        load_batch(0, 0, slice(1, 3))
        load_batch(0, 1)
        nc.sync.dma_start(out=w1_sb[:], in_=w1)
        load_batch(1, 0)
        load_batch(1, 1)
        load(2)
        nc.gpsimd.memset(g_rows[:], 0.0)
        nc.sync.dma_start(
            out=g_rows[0:4, :].rearrange("j (a r) -> j a r", r=8), in_=g.rearrange("(a j r) -> j a r", j=4, r=8)
        )
        for k, weight in enumerate((w2, w)):
            rows = weight.rearrange("(a j r) q -> j a r q", j=4, r=8)
            for j in range(4):
                nc.sync.dma_start(out=w_sb[:, k, j], in_=rows[j])
        nc.sync.dma_start(out=bias_sb[:], in_=bias)

        ident = keep.tile([P, P], F32, name="ident")
        make_identity(nc, ident[:])
        ident_b = keep.tile([P, P], BF16, name="ident_b", align_bytes=64)
        nc.scalar.activation(out=ident_b[:], in_=ident[:], func=ACT.Copy)

        wide = {}

        def slot_views(pair, i, lo, hi):
            if pair not in wide:
                wide[pair] = wide_pool.tile([P, 4, 2 * T], BF16, name="wide", align_bytes=64)
            return wide[pair][:, i, lo:hi], raw[pair][:, i, lo:hi].bitcast(FP8)

        def widen_scalar(pair, i, lo, hi):
            values, codes = slot_views(pair, i, lo, hi)
            nc.scalar.activation(out=values, in_=codes, func=ACT.Copy, scale=xs[:, i : i + 1])

        def widen_vector(pair, i, lo, hi):
            values, codes = slot_views(pair, i, lo, hi)
            nc.vector.tensor_scalar(out=values, in0=codes, scalar1=xs[:, i : i + 1], scalar2=None, op0=ALU.mult)

        def widen_slot(pair, i, lo=0):
            if pair <= LAST:
                widen_scalar(pair, i, lo, 2 * T - (RELEASE_COLUMNS if i == 3 else 0))

        w1_laid = keep.tile([P, 4 * PF], BF16, name="w1_laid", align_bytes=64)
        w1_codes = keep.tile([P, PF], U32, name="w1_codes", align_bytes=64)
        w1_scales = keep.tile([P, PF], U8, name="w1_scales", align_bytes=64)
        w_laid = keep.tile([P, 2, Q, 4], BF16, name="w_laid", align_bytes=64)
        w_codes = keep.tile([P, 2 * Q], U32, name="w_codes", align_bytes=64)
        w_scales = keep.tile([P, 2 * Q], U8, name="w_scales", align_bytes=64)

        w1_words = w1_sb[:].bitcast(F32)
        w1_turned = ps_h.tile([P, T], F32, name="h0")
        for half in (0, 1):
            nc.tensor.transpose(w1_turned[:, PF * half : PF * (half + 1)], w1_words[:, half : D // 2 : 2], ident[:])
        g_turned = ps_laid.tile([P, P], BF16, name="laid_ps")
        nc.tensor.transpose(g_turned[:], g_rows[:], ident_b[:])

        def lay_w1():
            nc.vector.tensor_copy(
                out=w1_laid[:].bitcast(F32).rearrange("p (f half) -> p f half", half=2),
                in_=w1_turned[:, 0 : 2 * PF].rearrange("p (half f) -> p f half", half=2),
            )

        def quantise_w1():
            nc.vector.quantize_mx(out=w1_codes[:].bitcast(FP8X4), scales=w1_scales[:], in_=w1_laid[:])

        def lay_w():
            nc.vector.tensor_copy(out=w_laid[:, 0], in_=w_sb[:, 0].rearrange("p j q -> p q j"))
            nc.vector.tensor_scalar(
                out=w_laid[:, 1], in0=w_sb[:, 1].rearrange("p j q -> p q j"),
                scalar1=-1.0, scalar2=None, op0=ALU.mult,
            )

        def quantise_w():
            nc.vector.quantize_mx(
                out=w_codes[:].bitcast(FP8X4), scales=w_scales[:], in_=w_laid[:].rearrange("p k q j -> p (k q j)")
            )

        lam128 = keep.tile([P, 1], F32, name="lam128")
        near_zero = keep.tile([P, 1], F32, name="near_zero")
        c = keep.tile([P, 1], F32, name="c")
        c_inv = keep.tile([P, 1], F32, name="c_inv")
        shift = keep.tile([P, 1], F32, name="shift")
        bias_c = keep.tile([P, Q], F32, name="bias_c")
        bias_ps = ps_bias.tile([P, Q], F32, name="bias_ps")

        def scale_lam():
            nc.vector.tensor_scalar(out=lam128[:], in0=lam_sb[:], scalar1=128.0, scalar2=None, op0=ALU.mult)

        def find_near_zero():
            nc.vector.tensor_scalar(
                out=near_zero[:], in0=lam128[:], scalar1=lam128[:], scalar2=TINY * TINY, op0=ALU.mult, op1=ALU.is_lt
            )

        def make_c():
            nc.vector.scalar_tensor_tensor(
                out=c[:], in0=near_zero[:], scalar=2 * TINY, in1=lam128[:], op0=ALU.mult, op1=ALU.add
            )

        def make_shift():
            nc.vector.scalar_tensor_tensor(
                out=shift[:], in0=lam_sb[:], scalar=1.0, in1=c_inv[:], op0=ALU.subtract, op1=ALU.mult
            )

        def scale_bias():
            nc.vector.tensor_scalar(out=bias_c[:], in0=bias_sb[:], scalar1=c_inv[:], scalar2=None, op0=ALU.mult)

        laid = {}
        by_batch = (0, LAST)

        def run_views(pair, lo, hi):
            if pair not in laid:
                laid[pair] = laid_pool.tile([P, 2 * BATCH_COLUMNS], BF16, name="laid", align_bytes=64)
            src = wide[pair][:].rearrange("p i (s j r) -> p s j r i", j=4, r=8)[:, lo // 2 : hi // 2]
            region, first = laid[pair][:], 0
            if pair in by_batch:
                b = lo // RUNS
                region, first = region[:, BATCH_COLUMNS * b : BATCH_COLUMNS * (b + 1)], RUNS * b
            dst = region.rearrange("p (j s r i) -> p s j r i", j=4, r=8, i=4)
            return src, dst[:, (lo - first) // 2 : (hi - first) // 2]

        def lay_vector(pair, lo, hi):
            src, dst = (ap.rearrange("p s j r i -> p j s i r") for ap in run_views(pair, lo, hi))
            nc.vector.tensor_copy(out=dst, in_=src)

        def lay_scalar(pair, lo, hi):
            src, dst = (ap.rearrange("p s j r i -> p s j i r") for ap in run_views(pair, lo, hi))
            nc.scalar.copy(out=dst, in_=src)

        def first_gpsimd_run(pair):
            return 2 * RUNS - gpsimd_runs(pair)

        def first_tensor_run(pair):
            return first_gpsimd_run(pair) - tensor_runs(pair)

        def release_gpsimd(pair):
            widen_vector(pair, 3, 2 * T - RELEASE_COLUMNS, 2 * T)
            src, dst = run_views(pair, first_gpsimd_run(pair), 2 * RUNS)
            nc.gpsimd.tensor_scalar(out=dst, in0=src, scalar1=1.0, scalar2=0.0, op0=ALU.mult, op1=ALU.add)

        laid_ps = {}

        def lay_tensor(pair):
            laid_ps[pair] = ps_laid.tile([P, 64 * tensor_runs(pair)], BF16, name="laid_ps")
            for lo, hi in ((0, TENSOR_RUNS), (TENSOR_RUNS, tensor_runs(pair))):
                src, dst = run_views(pair, first_tensor_run(pair) + lo, first_tensor_run(pair) + hi)
                nc.tensor.matmul(
                    laid_ps[pair][:, 64 * lo : 64 * hi].rearrange("p (t i) -> p t i", i=4), lhsT=ident_b[:],
                    rhs=src.rearrange("p s j r i -> p (s j r) i"), start=True, stop=True,
                )

        def copy_out_laid(pair):
            src, dst = run_views(pair, first_tensor_run(pair), first_gpsimd_run(pair))
            nc.vector.tensor_copy(
                out=dst.rearrange("p s j r i -> p s j (r i)"),
                in_=laid_ps[pair][:].rearrange("p (s j n) -> p s j n", j=4, n=32),
            )

        x_codes, x_scales, h0, h = {}, {}, {}, {}

        def quantise_x(pair, lo, hi):
            if pair not in x_codes:
                x_codes[pair] = code_pool.tile([P, 2 * T], U32, name="x_codes", align_bytes=64)
                x_scales[pair] = code_pool.tile([P, 2 * T], U8, name="x_scales", align_bytes=64)
            nc.vector.quantize_mx(
                out=x_codes[pair][:, lo // 4 : hi // 4].bitcast(FP8X4), scales=x_scales[pair][:, lo // 4 : hi // 4],
                in_=laid[pair][:, lo:hi],
            )

        def stage1(pair, b, tiles=range(4)):
            if (pair, b) not in h0:
                h0[pair, b] = ps_h.tile([P, T], F32, name="h0")
            for j in tiles:
                place = 4 * b + j if pair in by_batch else 2 * j + b
                cols = slice(P * place, P * (place + 1))
                nc.tensor.matmul_mx(
                    out=h0[pair, b][:, PF * j : PF * (j + 1)],
                    lhsT=x_codes[pair][:, cols].bitcast(FP8X4), lhsT_scale=x_scales[pair][:, cols],
                    rhs=w1_codes[:].bitcast(FP8X4), rhs_scale=w1_scales[:],
                    start=True, stop=True,
                )

        def gain(pair, b):
            if b == 0:
                h[pair] = h_pool.tile([P, 2, PF, 4], BF16, name="h", align_bytes=64)
            nc.vector.tensor_tensor(
                out=h[pair][:, b],
                in0=h0[pair, b][:].rearrange("p (j f) -> p f j", j=4),
                in1=g_sb[:].unsqueeze(1).to_broadcast([P, PF, 4]),
                op=ALU.mult,
            )

        ue, neg_max, total, offset, total_inv, work = {}, {}, {}, {}, {}, {}

        def stage2(part):
            pair, b0, n = part
            h_codes = h_pool.tile([P, n * PF], U32, name="h_codes", align_bytes=64)
            h_scales = h_pool.tile([P, n * PF], U8, name="h_scales", align_bytes=64)
            nc.vector.quantize_mx(
                out=h_codes[:].bitcast(FP8X4), scales=h_scales[:],
                in_=h[pair][:, b0 : b0 + n].rearrange("p b f j -> p (b f j)"),
            )
            ue[part] = ps_ue.tile([P, n, 2, Q], F32, name="ue")
            for k in range(n):
                cols = slice(PF * k, PF * (k + 1))
                nc.tensor.matmul_mx(
                    out=ue[part][:, k].rearrange("p a q -> p (a q)"),
                    lhsT=h_codes[:, cols].bitcast(FP8X4), lhsT_scale=h_scales[:, cols],
                    rhs=w_codes[:].bitcast(FP8X4), rhs_scale=w_scales[:],
                    start=True, stop=True,
                )

        scores, plain, rest = {}, {}, {}

        def stage2_alone(part):
            pair, b0, n = part
            h_codes = h_pool.tile([P, PF], U32, name="h_codes", align_bytes=64)
            h_scales = h_pool.tile([P, PF], U8, name="h_scales", align_bytes=64)
            nc.vector.quantize_mx(
                out=h_codes[:].bitcast(FP8X4), scales=h_scales[:], in_=h[pair][:, b0].rearrange("p f j -> p (f j)")
            )
            scores[part] = ps_laid.tile([P, 1, Q], F32, name="laid_ps")
            plain[part] = ps_h.tile([P, Q], F32, name="h0")
            for target, k in ((scores[part][:, 0], 1), (plain[part][:], 0)):
                cols = slice(Q * k, Q * (k + 1))
                nc.tensor.matmul_mx(
                    out=target, lhsT=h_codes[:].bitcast(FP8X4), lhsT_scale=h_scales[:],
                    rhs=w_codes[:, cols].bitcast(FP8X4), rhs_scale=w_scales[:, cols], start=True, stop=True,
                )

        def e_of(part):
            return scores[part][:] if part in scores else ue[part][:, :, 1]

        def plain_path(part):
            rest[part] = tail_pool.tile([P, Q], F32, name="rest")
            nc.vector.scalar_tensor_tensor(
                out=rest[part][:], in0=plain[part][:], scalar=shift[:], in1=bias_c[:], op0=ALU.mult, op1=ALU.subtract
            )

        def weigh_alone(part):
            nc.vector.tensor_tensor(out=work[part][:, 0], in0=work[part][:, 0], in1=plain[part][:], op=ALU.mult)

        def mix_alone(part):
            nc.vector.scalar_tensor_tensor(
                out=work[part][:, 0], in0=work[part][:, 0], scalar=total_inv[part][:], in1=rest[part][:],
                op0=ALU.mult, op1=ALU.subtract,
            )

        def row_max(part):
            neg_max[part] = tail_pool.tile([P, part[2]], F32, name="neg_max")
            nc.vector.tensor_reduce(out=neg_max[part][:], in_=e_of(part), axis=AX.X, op=ALU.min)

        def exps(part):
            total[part] = tail_pool.tile([P, part[2]], F32, name="total")
            work[part] = tail_pool.tile([P, part[2], Q], F32, name="work")
            for k in range(part[2]):
                nc.scalar.activation(
                    out=work[part][:, k], in_=e_of(part)[:, k], func=ACT.Exp,
                    bias=neg_max[part][:, k : k + 1], scale=-1.0, accum_out=total[part][:, k : k + 1],
                )

        def offsets(part):
            offset[part] = tail_pool.tile([P, part[2]], F32, name="offset")
            nc.scalar.activation(out=offset[part][:], in_=total[part][:], func=ACT.Copy, scale=shift[:])

        def invert(part):
            total_inv[part] = tail_pool.tile([P, part[2]], F32, name="total_inv")
            nc.vector.reciprocal(total_inv[part][:], total[part][:])

        def weigh(part):
            for k in range(part[2]):
                nc.vector.scalar_tensor_tensor(
                    out=work[part][:, k], in0=work[part][:, k], scalar=offset[part][:, k : k + 1],
                    in1=ue[part][:, k, 0], op0=ALU.subtract, op1=ALU.mult,
                )

        def mix(part):
            for k in range(part[2]):
                nc.vector.scalar_tensor_tensor(
                    out=work[part][:, k], in0=work[part][:, k], scalar=total_inv[part][:, k : k + 1],
                    in1=bias_ps[:], op0=ALU.mult, op1=ALU.add,
                )

        def finish(part):
            pair, b0, n = part
            result = tail_pool.tile([P, n, Q], F32, name="result", bufs=LAST + 2)
            nc.scalar.activation(out=result[:], in_=work[part][:], func=ACT.Tanh, scale=c[:])
            rows = slice(2 * pair + b0, 2 * pair + b0 + n)
            queue = nc.scalar if part == (LAST, 1, 1) else nc.sync
            queue.dma_start(out=out[rows].rearrange("b p q -> p b q"), in_=result[:])

        def whole(pair, stage):
            if pair >= 0:
                stage((pair, 0, 2))

        for b, row_step in enumerate((scale_lam, find_near_zero)):
            for i in range(4):
                widen = widen_vector if i < 3 - b else widen_scalar
                widen(0, i, b * T, (b + 1) * T)
            row_step()
        for i in range(4):
            widen_scalar(1, i, 0, T)
        for i in range(1, 4):
            widen_slot(1, i, T)
        lay_vector(0, 0, RUNS)
        make_c()
        lay_w1()
        lay_vector(0, RUNS, 2 * RUNS)
        nc.vector.reciprocal(c_inv[:], c[:])
        quantise_w1()
        widen_vector(1, 0, T, 2 * T)

        for n in range(LAST - 1):
            load(n + 3)
            widen_slot(n + 2, 0)
            whole(n - 3, finish)
            whole(n - 2, offsets)

            if n == 1:
                lay_w()
            if n > 0:
                lay_tensor(n + 1)
            if n == 1:
                scale_bias()
                quantise_w()
            whole(n - 1, stage2)
            if n == 0:
                quantise_x(0, 0, BATCH_COLUMNS)
                quantise_x(0, BATCH_COLUMNS, 2 * BATCH_COLUMNS)
            else:
                quantise_x(n, 0, 2 * BATCH_COLUMNS)
            stage1(n, 0)
            stage1(n, 1)
            if n == 0:
                lay_tensor(1)
                make_shift()
                nc.vector.tensor_copy(out=g_sb[:], in_=g_turned[:, 0:4])
            for i in range(1, 4):
                widen_slot(n + 2, i)
            whole(n - 2, invert)
            late = first_tensor_run(n + 1) - (EARLY_RUNS if n <= 1 else 0)
            if n <= 1:
                lay_vector(n + 1, late, first_tensor_run(n + 1))
            release_gpsimd(n + 1)
            lay_vector(n + 1, 0, late)
            if n == 1:
                nc.tensor.matmul(bias_ps[:], lhsT=ident[:], rhs=bias_c[:], start=True, stop=True)

            whole(n - 1, row_max)
            whole(n - 1, exps)
            whole(n - 2, weigh)
            gain(n, 0)
            if n > 1:
                copy_out_laid(n + 1)
            gain(n, 1)
            if n <= 1:
                copy_out_laid(n + 1)
            whole(n - 2, mix)

        n = LAST - 1
        whole(n - 2, offsets)
        lay_scalar(LAST, 0, RUNS)
        whole(n - 3, finish)
        whole(n - 1, stage2)
        whole(n - 2, invert)
        for half in range(2):
            if half == 1:
                release_gpsimd(LAST)
            quantise_x(n, half * BATCH_COLUMNS, (half + 1) * BATCH_COLUMNS)
            for b in range(2):
                stage1(n, b, range(2 * half, 2 * half + 2))
        whole(n - 1, row_max)
        whole(n - 1, exps)
        lay_scalar(LAST, RUNS, first_gpsimd_run(LAST))
        whole(n - 2, weigh)
        whole(n - 2, mix)
        whole(n - 1, offsets)
        whole(n - 2, finish)
        gain(n, 0)
        gain(n, 1)

        first, second = (LAST, 0, 1), (LAST, 1, 1)
        quantise_x(LAST, 0, BATCH_COLUMNS)
        stage1(LAST, 0)
        whole(LAST - 1, stage2)
        quantise_x(LAST, BATCH_COLUMNS, 2 * BATCH_COLUMNS)
        stage1(LAST, 1)
        whole(LAST - 2, invert)
        whole(LAST - 2, weigh)
        gain(LAST, 0)
        whole(LAST - 1, row_max)
        whole(LAST - 1, exps)
        gain(LAST, 1)
        stage2_alone(first)
        whole(LAST - 1, offsets)
        stage2_alone(second)
        whole(LAST - 2, mix)
        whole(LAST - 2, finish)
        whole(LAST - 1, invert)
        whole(LAST - 1, weigh)
        for part in (first, second):
            row_max(part)
            exps(part)
        whole(LAST - 1, mix)
        plain_path(first)
        plain_path(second)
        whole(LAST - 1, finish)
        invert(first)
        weigh_alone(first)
        invert(second)
        weigh_alone(second)
        for part in (first, second):
            mix_alone(part)
            finish(part)
